import numpy as np, ml_dtypes
CORES = [6,15,38,47]
N = 4
BF = ml_dtypes.bfloat16
P, M, C, I, D, S, SH = 512, 256, 256, 16, 1, 4, 7
J = I // D; U = 1 << SH; FILL = (P - M) // S + 2
def at(rng, t, e):
    b = e >> 4
    a = b + (((np.arange(16)[:, None] + rng.integers(0, 16, e.shape)) & 15) < (e & 15))
    sh = e.shape[:-2] + (8, e.shape[-1])
    z = np.floor((np.minimum(b, 127 - b) + 1) * rng.random(sh)).astype(np.int64) * (2 * rng.integers(0, 2, sh) - 1)
    a[..., 0::2, :] += z; a[..., 1::2, :] -= z
    return t + np.where(t < 128, 1, -1) * a
def lean(rng, t, e, m):
    a = (e >> 4) + (((np.arange(16)[:, None] + rng.integers(0, 16, e.shape)) & 15) < (e & 15))
    z = rng.integers(0, m + 1, e.shape[:-2] + (8, e.shape[-1]))
    a[..., 0::2, :] -= z; a[..., 1::2, :] += z
    return t + a
def far(rng, t, k):
    u = rng.integers(0, 16, t.shape[:-1] + (k,))
    return np.where(t < 128, 255 - u, u)
def parts(rng, dev):
    t = np.clip(rng.integers(0, 256, (1, 8, 16, 1)) + rng.integers(-dev, dev + 1, (N, 8, 16, 1)), 0, 255)
    e = U * np.repeat(np.arange(16), M) + rng.integers(0, U, (N, 8, 1, 16 * M))
    return {"t": t, "n": rng.integers(M >> 1, M + 1, (N, 8, 16)), "hs": at(rng, t, e), "x": at(rng, t, rng.integers(0, 16 * U, (N, 8, 1, C))),
            "dv": rng.integers(0, 256, (N, 8, 16, S * C)) >> rng.integers(0, 8, (N, 8, 1, S * C)), "te": rng.integers(0, 5, (N, 8))}
def pack(p):
    def b(v):
        return np.ascontiguousarray(v.reshape(N, 128, -1)).astype(np.float32).astype(BF)
    return {"hs": b(p["hs"]), "cn": p["n"].reshape(N, 128, 1).astype(np.int32), "x0": b(p["x"]), "tg": b(p["t"]), "dv": b(p["dv"]),
            "te": np.repeat(p["te"], 16, axis=1).reshape(N, 128, 1).astype(np.int32)}
def setup_inputs(rng):
    p = parts(rng, 4); t = p["t"]
    lo = rng.integers(0, 12, (N, 8, 1, 1)); wd = rng.choice(np.array([1, 4, 16]), (N, 8, 1, 1))
    e = np.minimum((lo * U + wd * U * rng.random((N, 8, 1, C))).astype(np.int64), 16 * U - 1)
    low = np.zeros((N, 8, 1, 1), bool); low[np.arange(N), rng.integers(0, 8, N)] = True
    e = np.where(low, rng.integers(0, U, e.shape), e); p["te"] = np.where(low[..., 0, 0], 0, p["te"])
    away = (rng.random(e.shape) < 0.125) & ~low
    p["x"] = np.where(away, far(rng, t, C), at(rng, t, e))
    p["hs"][..., 15 * M:] = np.where(rng.random((N, 8, 1, M)) < 0.25, far(rng, t, M), p["hs"][..., 15 * M:])
    return pack(p)
def setup_inputs_caps(rng):
    p = parts(rng, 0); p["te"] = 0 * p["te"]; p["dv"] = 0 * p["dv"]; kr = np.zeros((N, 8, 1, C), np.int64); ov = rng.integers(0, 15, 8)
    F = min(C, P >> 1); fk = rng.integers(3, 8, 8)
    for g in (2, 3):
        k = int(fk[g])
        goal = 2655 - ((97 * (I - 1) + 5 * (C - 1) + U) >> 1) - U * k
        p["t"][:, g] = at(rng, np.zeros((16, 1), np.int64), np.array([[goal]]))
        p["hs"][:, g] = at(rng, p["t"][:, g], U * np.repeat(np.arange(16), M) + rng.integers(0, U, (N, 1, 16 * M)))
        p["hs"][:, g, :, k * M:(k + 1) * M] = lean(rng, p["t"][:, g], U * k + rng.integers(1, U, (N, 1, M)), U * k >> 5)
    for r in range(N):
        for g in range(8):
            if g < 2:
                o = rng.permutation(16)
                kr[r, g, 0] = rng.permutation(np.concatenate([np.repeat(o[:3], FILL), rng.choice(o[3:9], C - 3 * FILL)]))
                p["n"][r, g, o[:3]] = P + np.array([0, -1, 1]) - S * FILL
            elif g < 4:
                k = int(fk[g])
                kr[r, g, 0] = rng.choice(np.delete(np.arange(16), k), C)
                kr[r, g, 0, rng.permutation(C)[:F]] = k
                p["n"][r, g, k] = P - F
            else:
                k = int(ov[g])
                kr[r, g, 0] = rng.permutation(np.concatenate([np.repeat(k, C - 4), np.repeat(k + 1, 4)]))
                p["n"][r, g, k] = M; p["n"][r, g, k + 1] = 1
    p["x"] = at(rng, p["t"], U * kr + rng.integers(0, U, kr.shape))
    for r in range(N):
        for g in (2, 3):
            k = int(fk[g]); c = np.flatnonzero(kr[r, g, 0] == k)
            p["x"][r, g][:, c] = lean(rng, p["t"][r, g], U * k + rng.integers(1, U, (1, len(c))), U * k >> 5)
            p["x"][r, g, :, int(c[-1])] = p["t"][r, g, :, 0] + (U * k >> 3) * (1 - (np.arange(16) & 1))
    return pack(p)
def setup_inputs_crowd(rng):
    p = parts(rng, 4); kr = rng.integers(0, 16, (N, 8, 1, 1)); kr[:, 0] = 0; kr[:, 1] = 15; kr[:, 2] = 15
    p["x"] = at(rng, p["t"], U * kr + rng.integers(0, U, (N, 8, 1, C)))
    p["n"] = np.where(np.arange(16) == kr[..., 0], M, p["n"])
    p["te"] = rng.choice(np.array([0, 0, 3, 1024]), (N, 8))
    t = 255 * rng.integers(0, 2, (N, 16, 1)); p["t"][:, 2] = t
    p["hs"][:, 2] = at(rng, t, U * np.repeat(np.arange(16), M) + rng.integers(0, U, (N, 1, 16 * M)))
    p["hs"][:, 2, :, 15 * M:] = far(rng, t, M)
    p["x"][:, 2] = np.where(np.arange(C) & 1, far(rng, t, C), 255 - t)
    return pack(p)
def setup_inputs_ties(rng):
    p = parts(rng, 0); t = p["t"]; lv = np.array([0, U >> 2, U >> 1, U - 1])
    p["hs"] = at(rng, t, U * np.repeat(np.arange(16), M) + rng.choice(lv, (N, 8, 1, 16 * M)))
    x = at(rng, t, U * rng.integers(0, 16, (N, 8, 1, C)) + rng.choice(lv, (N, 8, 1, C)))
    on = (rng.random((N, 8, 1, C)) < 0.5) & (np.arange(8)[:, None, None] >= 4)
    p["x"] = np.where(on, t, x); p["te"] = rng.integers(0, 9, (N, 8)); p["te"][:, :2] = 0
    p["dv"] = p["dv"] * rng.integers(0, 2, (N, 8, 1, S * C))
    back = np.where(t < 128, np.clip(2 * (p["x"] - t), 0, 255), 0)
    p["dv"][..., :C] = np.where(rng.random((N, 8, 1, C)) < 0.7, back, p["dv"][..., :C])
    y = rng.integers(240, 256, (16, 1)); y[0, 0] ^= int(np.add.reduce(y[:, 0])) & 1
    u = rng.integers(32, 41, (16, 1)); ty = int(np.add.reduce(y[:, 0])); tu = int(np.add.reduce(u[:, 0]))
    p["t"][:, 3] = u; p["hs"][:, 3] = y; p["dv"][:, 3] = 0
    for r in range(N):
        T, m = ((257, 8), (513, 4), (1021, 3), (1024, 2))[r & 3]
        e = ty - tu - T * m; v = ((tu + e - m) & 63) >> 1
        b = (e - v) // 15
        a = b + (((np.arange(15)[:, None] + rng.integers(0, 15, (1, C))) % 15) < e - v - 15 * b)
        z = rng.integers(0, b + 1, (7, C)) * (2 * rng.integers(0, 2, (7, C)) - 1)
        a[0:14:2] += z; a[1:14:2] -= z
        p["x"][r, 3] = np.concatenate([u[:15] + a, np.full((1, C), int(u[15, 0]) - v)], axis=0); p["te"][r, 3] = T
    return pack(p)
def setup_inputs_alike(rng):
    p = parts(rng, 4)
    p["x"] = np.repeat(at(rng, p["t"], rng.integers(0, 16 * U, (N, 8, 1, 1))), C, axis=3)
    p["n"] = rng.choice(np.array([1, 2, 3, M]), (N, 8, 16))
    p["hs"] = p["hs"][..., np.arange(16 * M) >> 2 << 2]
    return pack(p)
def setup_inputs_spread(rng):
    def un(*sh):
        return np.floor(np.exp2(8 * rng.random(sh[:-2] + (1, sh[-1]))) * rng.random(sh)).astype(np.int64)
    p = {"t": rng.integers(0, 256, (N, 8, 16, 1)), "hs": un(N, 8, 16, 16 * M), "x": un(N, 8, 16, C), "dv": un(N, 8, 16, S * C)}
    p["n"] = 1 + np.floor(M * rng.random((N, 8, 16)) ** 3).astype(np.int64)
    p["te"] = np.floor(np.exp2(10 * rng.random((N, 8)))).astype(np.int64) * (rng.random((N, 8)) < 0.75)
    return pack(p)
def check_inputs(d):
    bad = []
    for k, lo, hi in (("hs", 0, 255), ("cn", 1, M), ("x0", 0, 255), ("tg", 0, 255), ("dv", 0, 255), ("te", 0, 1024)):
        v = np.asarray(d[k]).astype(np.float64)
        if not (np.all(v >= lo) and np.all(v <= hi) and np.all(v == np.floor(v))): bad.append("whole numbers and range of " + k)
    v = np.asarray(d["te"]).reshape(N, 8, 16)
    if not np.all(v == v[:, :, :1]): bad.append("te alike in a group")
    return bad
def num(a, k):
    return a.astype(np.float32).astype(np.int64).reshape(N, 8, 16, k)
def energy(z, t):
    return np.add.reduce(np.abs(z - t), axis=-2)
def reference(hs, cn, x0, tg, dv, te):
    x = num(x0, C); goal = num(tg, 1); mv = num(dv, S * C); n = cn.astype(np.int64).reshape(N, 8, 16); T = te.astype(np.int64).reshape(N, 8, 16)[:, :, :1]
    H = np.zeros((N, 8, 16, 16, P), np.int64); H[..., :M] = num(hs, 16 * M).reshape(N, 8, 16, 16, M); H = H.reshape(N, 8, 16, 16 * P)
    cs = np.arange(C)
    for t in range(S):
        E = energy(x, goal); k = np.minimum(15, E >> SH); s = np.add.reduce(x, axis=2)
        bound = E + T * (s & 63); new = []
        for r in range(N):
            ys = []
            for d in range(D):
                q = (r + 1 + d) % N; i = d * J + np.arange(J)
                w = (s[r][:, None, :] + 97 * i[None, :, None] + 31 * t + 5 * cs) & 4095
                h = ((w * w >> 7) + w) & 4095
                nk = np.take_along_axis(n[q], k[r], 1)
                col = P * k[r][:, None, :] + (h * nk[:, None, :] >> 12)
                ys.append(np.take_along_axis(H[q], col.reshape(8, 1, J * C), 2).reshape(8, 16, J, C))
            ys = np.concatenate(ys, axis=2)
            dist = np.add.reduce(np.abs(ys - x[r][:, :, None, :]), axis=1)
            best = np.argmax(dist, axis=1)
            y = np.take_along_axis(ys, best[:, None, None, :], 2)[:, :, 0, :]
            z = np.abs(x[r] - mv[r][..., t * C:(t + 1) * C])
            oky = energy(y, goal[r]) <= bound[r]; okz = energy(z, goal[r]) <= bound[r]
            new.append(np.where(oky[:, None, :], y, np.where(okz[:, None, :], z, x[r])))
        x = np.stack(new)
        k = np.minimum(15, energy(x, goal) >> SH)
        eq = (k[:, :, None, :] == np.arange(16)[:, None]).astype(np.int64)
        place = np.take_along_axis(n[..., None] + np.add.accumulate(eq, axis=3) - eq, k[:, :, None, :], 2)[:, :, 0, :]
        for r in range(N):
            for g in range(8):
                m = place[r, g] < P
                H[r, g][:, (P * k[r, g] + place[r, g])[m]] = x[r, g][:, m]
        n = np.minimum(P, n + np.add.reduce(eq, axis=3))
    return {"yx": x.reshape(N, 128, C).astype(np.float32).astype(BF), "yn": n.reshape(N, 128, 1).astype(np.float32)}

@@ -1,0 +1,503 @@
+import numpy as np
+from concourse.bass import DstId, RemoteDMATransfer
+from concourse.mybir import dt, AluOpType, AxisListType, ActivationFunctionType
+
+OP = AluOpType
+AF = ActivationFunctionType
+C = 256
+RS = 768
+ST = 4
+CH = {"V0": (0, 4, "V"), "S0": (4, 4, "S"), "V1": (8, 4, "V"), "V2": (12, 4, "V")}
+EARLY = 192
+XR_S = 6
+
+SCRATCH = {
+    "st": ("sbuf", [128, 264], "bfloat16"), "sdv": ("sbuf", [128, 1024], "bfloat16"), "si": ("sbuf", [128, 2], "int32"),
+    "l0": ("sbuf", [128, 264], "bfloat16"), "ldv": ("sbuf", [128, 1024], "bfloat16"), "li": ("sbuf", [128, 2], "int32"),
+    "win": ("sbuf", [128, 16 * RS], "bfloat16"),
+    "lx": ("sbuf", [128, ST * C], "bfloat16"), "lc": ("sbuf", [128, ST * 20], "float32"), "cs": ("sbuf", [128, ST * 20], "float32"),
+    "x": ("sbuf", [128, 5 * C], "bfloat16"), "xr": ("sbuf", [128, ST * 4096], "bfloat16"),
+    "d": ("sbuf", [128, ST * 4096], "bfloat16"), "ad": ("sbuf", [128, ST * 16, 256], "bfloat16"), "yb": ("sbuf", [128, ST * 1024], "bfloat16"),
+    "off": ("sbuf", [128, ST * C], "uint16"), "lu": ("sbuf", [128, ST * 16], "uint16"), "sel": ("sbuf", [128, ST * 16], "uint16"),
+    "km": ("sbuf", [128, ST * C], "int32"), "ka": ("sbuf", [128, ST * 16], "int32"),
+    "ax": ("sbuf", [128, 5 * C], "bfloat16"), "gt": ("sbuf", [128, 5 * C], "float16"), "eq": ("sbuf", [128, 5 * C], "float16"),
+    "nn": ("sbuf", [128, 5 * C], "float32"), "pn": ("sbuf", [128, 5 * C], "float16"),
+    "sg": ("sbuf", [128, ST * C], "bfloat16"), "sq": ("sbuf", [128, ST * C], "float32"), "hd": ("sbuf", [128, ST * C], "int32"), "h": ("sbuf", [128, ST * C], "int32"),
+    "r": ("sbuf", [128, ST * C], "float16"), "sm": ("sbuf", [128, ST * C], "float16"),
+    "z": ("sbuf", [128, ST * C], "bfloat16"), "az": ("sbuf", [128, ST * C], "bfloat16"), "okz": ("sbuf", [128, ST * C], "bfloat16"),
+    "pz": ("sbuf", [128, ST * C], "bfloat16"), "zx": ("sbuf", [128, ST * C], "bfloat16"),
+    "y": ("sbuf", [128, ST * C], "bfloat16"), "ay": ("sbuf", [128, ST * C], "bfloat16"), "oky": ("sbuf", [128, ST * C], "bfloat16"), "pr": ("sbuf", [128, ST * C], "bfloat16"),
+    "v": ("sbuf", [128, ST * C], "float32"), "pp": ("sbuf", [128, ST * C], "float16"), "wn": ("sbuf", [128, ST * 128], "float16"),
+    "i3": ("sbuf", [128, 128], "int32"), "i4": ("sbuf", [128, 128], "int32"), "ic": ("sbuf", [128, 256], "int32"), "ip": ("sbuf", [128, 1], "int32"),
+    "iq": ("sbuf", [128, 1], "int32"), "t1": ("sbuf", [128, 128], "float32"), "t2": ("sbuf", [128, 128], "float32"), "t3": ("sbuf", [128, 128], "float32"), "t4": ("sbuf", [128, 128], "float32"),
+    "cb": ("sbuf", [128, 7 * 128], "bfloat16"), "cf": ("sbuf", [128, 6 * 128], "float16"),
+    "s4": ("sbuf", [128, 144], "bfloat16"), "s1": ("sbuf", [128, 144], "float16"), "s7": ("sbuf", [128, 144], "float16"),
+    "cc": ("sbuf", [128, 256], "bfloat16"), "co": ("sbuf", [128, 64], "int32"), "ia": ("sbuf", [128, 64], "int32"), "k1": ("sbuf", [128, 64], "bfloat16"), "k2": ("sbuf", [128, 64], "bfloat16"),
+    "mk": ("sbuf", [128, 64], "float32"), "one": ("sbuf", [128, 256], "float32"), "col": ("sbuf", [128, 32], "float32"),
+}
+for _k in range(8):
+    SCRATCH["b%d" % _k] = ("psum", [128, 512], "float32")
+SEMAPHORES = (["qV", "qS", "qP", "qG", "sx", "si", "sdv0", "sdv1", "hs", "rx", "rdv0", "ri", "rdv1", "ls", "oy", "on"]
+              + ["%s%d" % (k, t) for k in ("ra", "rb", "rc") for t in range(ST)])
+BONES, NB, ID, NID, I5, I2048 = [128 * k for k in range(6)]
+F1, F768, FI, FD, FM64, FT = [128 * k for k in range(6)]
+NTG, THR, TT, N0, NM, BA, BB, Q16 = 0, 1, 2, 3, 4, 12, 16, 20
+
+
+def rank_program(g, core, T, topo):
+    rank = T.rank_of(core)
+    if rank is None:
+        return
+    N = len(T.cores)
+    prev, nxt = T.cores[(rank - 1) % N], T.cores[(rank + 1) % N]
+    Q = {"V": g.vector, "S": g.scalar, "P": g.tensor, "G": g, "Y": g.sync}
+    cnt = {"V": 0, "S": 0, "P": 0, "G": 0}
+    seen = {k: {} for k in Q}
+    clock, hist, local = {}, {}, [0]
+
+    def need(E, tok):
+        if seen[E].get(tok[0], 0) >= tok[1]:
+            return
+        Q[E].wait_ge(T.sem[tok[0]], tok[1])
+        for s, v in clock.get(tok, {tok[0]: tok[1]}).items():
+            if seen[E].get(s, 0) < v:
+                seen[E][s] = v
+
+    def deps(E, reads, writes):
+        toks = {}
+        for wr, lst in ((False, reads), (True, writes)):
+            for (b, c0, c1, ln) in lst:
+                bank = SCRATCH[b][0] == "psum"
+                for (w, e, a0, a1, l2, tok) in hist.get(b, []):
+                    hit = a0 < c1 and c0 < a1 and (ln is None or l2 is None or ln == l2)
+                    if e == E:
+                        need_it = hit and E != "P" and w
+                    else:
+                        need_it = bank or (hit and (w or wr))
+                    if need_it and toks.get(tok[0], 0) < tok[1]:
+                        toks[tok[0]] = tok[1]
+        for s in sorted(toks):
+            need(E, (s, toks[s]))
+
+    def note(E, tok, reads, writes):
+        for wr, lst in ((False, reads), (True, writes)):
+            for (b, c0, c1, ln) in lst:
+                hist.setdefault(b, []).append((wr, E, c0, c1, ln, tok))
+
+    def op(E, call, reads, writes):
+        deps(E, reads, writes)
+        cnt[E] += 1
+        tok = ("q" + E, cnt[E])
+        call().then_inc(T.sem[tok[0]], 1)
+        ck = dict(seen[E])
+        ck[tok[0]] = tok[1]
+        clock[tok] = ck
+        note(E, tok, reads, writes)
+
+    def A(b, c0=0, n=1, step=1, lane=None):
+        ap = T[b][:, c0:c0 + n] if step == 1 else T[b][:, c0:c0 + (n - 1) * step + 1:step]
+        return (ap, [(b, c0, c0 + (n - 1) * step + 1, lane)])
+
+    def ind(win, off):
+        return (win[0].indirect(off[0]), win[1] + off[1])
+
+    def sc(s, rd):
+        if isinstance(s, tuple):
+            rd.extend(s[1])
+            return s[0]
+        return s
+
+    def tt(o, a, b, f):
+        op("V", lambda: g.vector.tensor_tensor(o[0], a[0], b[0], f), a[1] + b[1], o[1])
+
+    def ts(o, a, s1, f1, s2=None, f2=None):
+        rd = list(a[1])
+        p1 = sc(s1, rd)
+        if f2 is None:
+            op("V", lambda: g.vector.tensor_scalar(o[0], a[0], p1, None, f1), rd, o[1])
+        else:
+            p2 = sc(s2, rd)
+            op("V", lambda: g.vector.tensor_scalar(o[0], a[0], p1, p2, f1, f2), rd, o[1])
+
+    def cp(o, a):
+        op("V", lambda: g.vector.tensor_copy(o[0], a[0]), a[1], o[1])
+
+    def scan(o, d0, d1, init, f0, f1):
+        rd = d0[1] + d1[1]
+        i0 = sc(init, rd)
+        op("V", lambda: g.vector.tensor_tensor_scan(o[0], d0[0], d1[0], i0, f0, f1), rd, o[1])
+
+    def act(o, a, f, bias=0.0, scale=1.0):
+        rd = list(a[1])
+        b0 = sc(bias, rd)
+        op("S", lambda: g.scalar.activation(o[0], a[0], f, b0, scale), rd, o[1])
+
+    def mm(o, l, r, start, stop):
+        op("P", lambda: g.tensor.matmul(o[0], l[0], r[0], start, stop), l[1] + r[1], o[1])
+
+    def mms(o, pairs):
+        for k, (l, r) in enumerate(pairs):
+            mm(o, l, r, k == 0, k == len(pairs) - 1)
+
+    def dma(E, o_ap, i_ap, sem, total, reads, writes):
+        deps(E, reads, writes)
+        Q[E].dma_start(o_ap, i_ap).then_inc(T.sem[sem], 16)
+        note("dma", (sem, total), reads, writes)
+
+    def remote(dst, b, c0, n, srcb, s0, rsem):
+        src = A(srcb, s0, n)
+        deps("G", src[1], [])
+        rid, pid, _ = topo.addr(dst)
+        g.remote_dma(T[b][:, c0:c0 + n], src[0], T.sem[rsem], T.sem["ls"], pid, rid, topo.mask(core, dst))
+        local[0] += len(topo.engines(core, dst))
+
+    def arrives(src, b, c0, n, rsem):
+        note("net", (rsem, len(topo.engines(src, core))), [], [(b, c0, c0 + n, None)])
+
+    def CB(k):
+        return A("cb", k, 128)
+
+    def CF(k):
+        return A("cf", k, 128)
+
+    def COL(k):
+        return A("col", k, 1)
+
+    def X(t, c0=0, n=C):
+        return A("l0", c0, n) if t == 0 else A("x", t * C + c0, n)
+
+    dma("Y", T.st[:, 0:256], T.x0[:], "sx", 32, [], [("st", 0, 256, None)])
+    dma("S", T.st[:, 256:257], T.tg[:], "sx", 32, [], [("st", 256, 257, None)])
+    dma("S", T.si[:, 0:1], T.te[:], "si", 32, [], [("si", 0, 1, None)])
+    dma("S", T.si[:, 1:2], T.cn[:], "si", 32, [], [("si", 1, 2, None)])
+    dma("Y", T.sdv[:, 0:256], T.dv[:, 0:256], "sdv0", 16, [], [("sdv", 0, 256, None)])
+    for q in range(16):
+        dma("Y" if q % 2 == 0 else "S", T.win[:, q * RS:q * RS + 256], T.hs[:, q * 256:(q + 1) * 256], "hs", 256, [], [("win", q * RS, q * RS + 256, None)])
+    dma("Y", T.sdv[:, 256:1024], T.dv[:, 256:1024], "sdv1", 16, [], [("sdv", 256, 1024, None)])
+
+    op("G", lambda: g.iota(T.i4[:], [[-16, 8], [0, 16]], 0, 1), [], [("i4", 0, 128, None)])
+    op("G", lambda: g.iota(T.ip[:], [[0, 1]], 0, 1), [], [("ip", 0, 1, None)])
+    op("G", lambda: g.iota(T.i3[:], [[-1, 128]], 0, 1), [], [("i3", 0, 128, None)])
+    op("G", lambda: g.iota(T.ic[:], [[1, 256]], 0, 0), [], [("ic", 0, 256, None)])
+    remote(nxt, "l0", 0, 264 if False else 257, "st", 0, "rx")
+    remote(nxt, "ldv", 0, 256, "sdv", 0, "rdv0")
+    remote(nxt, "li", 0, 2, "si", 0, "ri")
+    remote(nxt, "ldv", 256, 768, "sdv", 256, "rdv1")
+    arrives(prev, "l0", 0, 257, "rx")
+    arrives(prev, "ldv", 0, 256, "rdv0")
+    arrives(prev, "li", 0, 2, "ri")
+    arrives(prev, "ldv", 256, 768, "rdv1")
+    for t in range(ST):
+        arrives(nxt, "lx", t * C, EARLY, "ra%d" % t)
+        arrives(nxt, "lx", t * C + EARLY, C - EARLY, "rb%d" % t)
+        if t < ST - 1:
+            arrives(nxt, "lc", t * 20, 17, "rc%d" % t)
+        else:
+            arrives(nxt, "lc", t * 20 + 16, 1, "rc%d" % t)
+
+    I3, I4 = A("i3", 0, 128), A("i4", 0, 128)
+    T1, T2, T3, T4 = A("t1", 0, 128), A("t2", 0, 128), A("t3", 0, 128), A("t4", 0, 128)
+    IQ = A("iq", 0, 1)
+    ts(T1, I4, 0, OP.is_ge)
+    ts(T2, I4, 15, OP.is_le)
+    ts(IQ, A("ip", 0, 1), 15, OP.bitwise_and)
+    tt(CB(BONES), T1, T2, OP.mult)
+    ts(CB(ID), I3, 0, OP.is_equal)
+    ts(CB(I5), I3, 0, OP.is_equal, 5.0, OP.mult)
+    ts(CB(I2048), I3, 0, OP.is_equal, -2048.0, OP.mult)
+    cp(A("cc", 0, 256), A("ic", 0, 256))
+    ts(COL(THR), IQ, 128.0, OP.mult)
+    for t in range(ST):
+        ts(COL(BA + t), IQ, -97.0, OP.mult, 1455.0 + 31 * t - 4095.5, OP.add)
+        ts(COL(BB + t), IQ, -97.0 / 16, OP.mult, (1455.0 + 31 * t - 2048 + 64) / 16, OP.add)
+    ts(COL(Q16), IQ, 16.0, OP.mult)
+    ts(T3, I3, 1, OP.is_equal, -1.0, OP.mult)
+    ts(CF(F1), CB(BONES), 1.0, OP.mult)
+    tt(T4, T3, CB(BONES), OP.mult)
+    ts(CF(F768), CB(BONES), float(RS), OP.mult)
+    ts(CF(FI), I3, 0, OP.is_equal)
+    tt(CF(FD), T4, CB(ID), OP.add)
+    ts(CF(FM64), I3, 0, OP.is_equal, -64.0, OP.mult)
+    ts(CB(NB), CB(BONES), -1.0, OP.mult)
+    ts(CB(NID), I3, 0, OP.is_equal, -1.0, OP.mult)
+    for b, w in (("s4", 4096.0), ("s1", 1.0), ("s7", float(RS))):
+        ts(A(b, 0, 144), A("ic", 0, 144), 0.0, OP.mult)
+    ts(A("co", 0, 64), A("ic", 0, 64), 15, OP.bitwise_and)
+    ts(A("ia", 0, 64), A("ic", 0, 64), 4, OP.arith_shift_right)
+    for b, w in (("s4", 4096.0), ("s1", 1.0), ("s7", float(RS))):
+        ts(A(b, 15, 8, 16), A("cb", BONES, 8, 16), w, OP.mult)
+    ts(A("k2", 0, 64), A("co", 0, 64), COL(Q16), OP.add)
+    ts(A("k1", 0, 64), A("ia", 0, 64), 256.0, OP.mult)
+    ts(A("mk", 0, 64), A("co", 0, 64), 1.0, OP.min)
+    op("V", lambda: g.vector.memset(T.one[:], 1.0), [], [("one", 0, 256, None)])
+
+    def absx(t, c0, n):
+        act(A("ax", t * C + c0, n), X(t, c0, n), AF.Abs, COL(NTG))
+
+    def ring(t, c0, n):
+        mms(A("b6", c0, n), [(CB(BONES), A("ax", t * C + c0, n))])
+        ts(A("gt", t * C + c0, n), A("b6", c0, n), COL(THR), OP.is_ge)
+        mms(A("b7", c0, n), [(CF(FD), A("gt", t * C + c0, n))])
+
+    def place(t, c0, n):
+        scan(A("nn", t * C + c0, n), A("one", 0, n), A("b7", c0, n), COL(NM + t - 1) if c0 == 0 else A("nn", t * C + c0 - 1, 1), OP.mult, OP.add)
+        if t < ST:
+            tt(A("pn", t * C + c0, n), A("nn", t * C + c0, n), A("b7", c0, n), OP.mult)
+
+    def list_rings(t):
+        for p in range(16):
+            mm(A("b6", 256, 16), A("s7", 15 - p, 128), A("gt", t * C + p, 16, 16), p == 0, False)
+
+    def list_places(t):
+        for p in range(16):
+            mm(A("b6", 256, 16), A("s1", 15 - p, 128), A("pn", t * C + p, 16, 16), False, p == 15)
+
+    def counts(t):
+        last = A("nn", t * C + C - 1, 1)
+        ts(A("cs", (t - 1) * 20 + 16, 1), last, 1.0, OP.add, 512.0, OP.min)
+        if t < ST:
+            ts(COL(NM + t), last, 511.0, OP.min)
+
+    def eq16(t):
+        cp(A("eq", t * C, C), A("b7", 0, C))
+
+    def w_first(t):
+        mms(A("b0", 0, C), [(CB(BONES), X(t)), (CB(I5), A("cc", 0, C))])
+        act(A("sg", t * C, C), A("b0", 0, C), AF.Sign, COL(BA + t))
+        mms(A("b1", 0, C), [(CB(BONES), X(t)), (CB(I5), A("cc", 0, C)), (CB(I2048), A("sg", t * C, C))])
+
+    def w_square(t):
+        act(A("sq", t * C, C), A("b1", 0, C), AF.Square, COL(BB + t), 1.0 / 16)
+
+    def h_round(t):
+        ts(A("hd", t * C, C), A("sq", t * C, C), 2.0, OP.mult, -4156.0 / 128, OP.add)
+
+    def h_mod(t):
+        ts(A("h", t * C, C), A("hd", t * C, C), 4095, OP.bitwise_and)
+
+    def s_div(t):
+        mms(A("b2", 0, C), [(CB(BONES), X(t))])
+        ts(A("r", t * C, C), A("b2", 0, C), 1.0 / 64, OP.mult, 1026.0 - 63.0 / 128, OP.add)
+        mms(A("b2", 256, C), [(CB(BONES), X(t)), (CF(FM64), A("r", t * C, C))])
+
+    def s_mod(t):
+        ts(A("sm", t * C, C), A("b2", 256, C), 1026.0 * 64, OP.add)
+
+    def z_make(t):
+        mms(A("b3", 0, C), [(CB(ID), X(t)), (CB(NID), A("ldv", t * C, C))])
+        act(A("z", t * C, C), A("b3", 0, C), AF.Abs)
+        act(A("az", t * C, C), A("z", t * C, C), AF.Abs, COL(NTG))
+
+    def z_ok(t):
+        mms(A("b4", 0, C), [(CB(BONES), A("az", t * C, C)), (CB(NB), A("ax", t * C, C)), (CF(FT), A("sm", t * C, C))])
+        mms(A("b5", 0, C), [(CB(ID), A("z", t * C, C)), (CB(NID), X(t))])
+        ts(A("okz", t * C, C), A("b4", 0, C), 0.0, OP.is_le)
+
+    def z_pick(t):
+        tt(A("pz", t * C, C), A("okz", t * C, C), A("b5", 0, C), OP.mult)
+        mms(A("b3", 256, C), [(CB(ID), X(t)), (CB(ID), A("pz", t * C, C))])
+
+    def z_store(t):
+        act(A("zx", t * C, C), A("b3", 256, C), AF.Copy)
+
+    def xrep(t, k):
+        o = A("xr", t * 4096 + k, C, 16, k)
+        if k < 16 - XR_S:
+            cp(o, X(t))
+        else:
+            act(o, X(t), AF.Copy)
+
+    def weights(t):
+        ts(A("wn", t * 128, 128), CF(F1), COL(N0) if t == 0 else A("lc", (t - 1) * 20 + 16, 1), OP.mult)
+        mms(A("b0", 0, C), [(A("wn", t * 128, 128), A("eq", t * C, C))])
+
+    def append(t):
+        cp(A("lu", t * 16, 16), A("lc", t * 20, 16))
+        cp(ind(A("win", 0, 16 * RS), A("lu", t * 16, 16)), A("lx", t * C, C))
+
+    def append_list(t):
+        cp(A("lu", t * 16, 16), A("lc", t * 20, 16))
+
+    def append_scatter(t):
+        w, o = A("win", 0, 16 * RS), A("lu", t * 16, 16)
+        src = A("lx", t * C, C)
+        op("V", lambda: g.vector.tensor_copy(w[0].indirect(o[0]), src[0]), src[1] + o[1], w[1])
+
+    def prod(t):
+        tt(A("v", t * C, C), A("h", t * C, C), A("b0", 0, C), OP.mult)
+
+    def floor_place(t, half):
+        c0 = 128 * half
+        ts(A("pp", t * C + c0, 128), A("v", t * C + c0, 128), 1.0 / 4096, OP.mult, 1026.0 - 2047.5 / 4096, OP.add)
+        mms(A("b%d" % (1 + 6 * half), c0, 128), [(CF(FI), A("pp", t * C + c0, 128)), (CF(F768), A("gt", t * C + c0, 128))])
+
+    def offsets(t, half):
+        c0 = 128 * half
+        ts(A("off", t * C + c0, 128), A("b%d" % (1 + 6 * half), c0, 128), -1026.0 - RS, OP.add)
+
+    def gather(t, k):
+        a0, al, e = CH[k]
+        n = 256 * al
+        src = ind(A("win", 0, 16 * RS), A("off", t * C + 16 * a0, 16 * al))
+        if e == "V":
+            tt(A("d", t * 4096 + 256 * a0, n), src, A("xr", t * 4096 + 256 * a0, n), OP.subtract)
+        else:
+            act(A("yb", t * 1024, n), src, AF.Copy)
+
+    def absd(t, k, lo, hi):
+        a0, al, e = CH[k]
+        for j in range(lo, hi):
+            o = (T.ad[:, t * 16 + a0 + j, :], [("ad", (t * 16 + a0 + j) * 256, (t * 16 + a0 + j + 1) * 256, None)])
+            if e == "V":
+                src = A("d", t * 4096 + 256 * (a0 + j), 256)
+            else:
+                src = A("b%d" % (2 + j // 2), 256 * (j % 2), 256)
+                if j % 2 == 0:
+                    mms(A("b%d" % (2 + j // 2), 0, 512), [(CB(ID), A("yb", t * 1024 + 256 * j, 512)), (CB(NID), A("xr", t * 4096 + 256 * (a0 + j), 512))])
+            act(o, src, AF.Abs)
+
+    KB = {"V0": "b0", "S0": "b1", "V1": "b0", "V2": "b1"}
+
+    def key(t, k):
+        a0, al, e = CH[k]
+        n = 16 * al
+        o = A(KB[k], 0, n)
+        mm(o, CB(ID), A("k1", 0, n), True, False)
+        mm(o, CB(ID), A("k2", 0, n), False, False)
+        for p in range(16):
+            r = (T.ad[:, t * 16 + a0:t * 16 + a0 + al, 16 * p:16 * p + 16], [("ad", (t * 16 + a0) * 256, (t * 16 + a0 + al) * 256, None)])
+            mm(o, A("s4", 15 - p, 128), r, False, p == 15)
+
+    def choose(t, k):
+        a0, al, e = CH[k]
+        n, c0 = 16 * al, t * C + 16 * a0
+        scan(A("km", c0, n), A("mk", 0, n), A(KB[k], 0, n), 0.0, OP.mult, OP.max)
+        ts(A("ka", t * 16 + a0, al), A("km", c0 + 15, al, 16), 4095, OP.bitwise_and)
+        cp(A("sel", t * 16 + a0, al), A("ka", t * 16 + a0, al))
+        if e == "V":
+            tt(A("y", c0, n), ind(A("d", t * 4096 + 256 * a0, 256 * al), A("sel", t * 16 + a0, al)), X(t, 16 * a0, n), OP.add)
+        else:
+            cp(A("y", c0, n), ind(A("yb", t * 1024, 256 * al), A("sel", t * 16 + a0, al)))
+        act(A("ay", c0, n), A("y", c0, n), AF.Abs, COL(NTG))
+        mms(A("b4", 16 * a0, n), [(CB(NB), A("ax", c0, n)), (CF(FT), A("sm", c0, n)), (CB(BONES), A("ay", c0, n))])
+        mms(A("b5", 16 * a0, n), [(CB(ID), A("y", c0, n)), (CB(NID), A("zx", c0, n))])
+        mms(A("b5", 256 + 16 * a0, n), [(CB(ID), A("zx", c0, n))])
+
+    def decide(t, k):
+        a0, al, e = CH[k]
+        n, c0 = 16 * al, t * C + 16 * a0
+        ts(A("oky", c0, n), A("b4", 16 * a0, n), 0.0, OP.is_le)
+        tt(A("pr", c0, n), A("oky", c0, n), A("b5", 16 * a0, n), OP.mult)
+        tt(X(t + 1, 16 * a0, n), A("pr", c0, n), A("b5", 256 + 16 * a0, n), OP.add)
+        if t < ST or True:
+            absx(t + 1, 16 * a0, n)
+
+    ts(COL(NTG), A("l0", 256, 1), -1.0, OP.mult)
+    cp(COL(N0), A("si", 1, 1))
+    absx(0, 0, C)
+    w_first(0)
+    for k in range(16 - XR_S):
+        if k < 2:
+            xrep(0, k)
+    ring(0, 0, C)
+    w_square(0)
+    eq16(0)
+    weights(0)
+    h_round(0)
+    h_mod(0)
+    prod(0)
+    floor_place(0, 0)
+    floor_place(0, 1)
+    for k in range(2, 16):
+        xrep(0, k)
+    offsets(0, 0)
+    offsets(0, 1)
+
+    def z_part(t):
+        s_div(t)
+        z_make(t)
+        s_mod(t)
+        z_ok(t)
+        z_pick(t)
+        z_store(t)
+
+    for t in range(ST):
+        gather(t, "V0")
+        gather(t, "S0")
+        if t == 0:
+            cp(COL(TT), A("li", 0, 1))
+            ts(COL(NM), A("li", 1, 1), -1.0, OP.add)
+            ts(CF(FT), CB(ID), COL(TT), OP.mult, -1.0, OP.mult)
+        gather(t, "V1")
+        absd(t, "V0", 0, 4)
+        key(t, "V0")
+        if t == 0:
+            z_part(0)
+        absd(t, "S0", 0, 4)
+        key(t, "S0")
+        choose(t, "V0")
+        gather(t, "V2")
+        absd(t, "V1", 0, 4)
+        decide(t, "V0")
+        key(t, "V1")
+        absd(t, "V2", 0, 4)
+        choose(t, "S0")
+        choose(t, "V1")
+        decide(t, "S0")
+        key(t, "V2")
+        decide(t, "V1")
+        remote(prev, "lx", t * C, EARLY, "x", (t + 1) * C, "ra%d" % t)
+        u = t + 1
+        ring(u, 0, EARLY)
+        choose(t, "V2")
+        place(u, 0, EARLY)
+        decide(t, "V2")
+        remote(prev, "lx", t * C + EARLY, C - EARLY, "x", u * C + EARLY, "rb%d" % t)
+        ring(u, EARLY, C - EARLY)
+        if u < ST:
+            list_rings(u)
+            w_first(u)
+            xrep(u, 0)
+            place(u, EARLY, C - EARLY)
+            list_places(u)
+            counts(u)
+            w_square(u)
+            xrep(u, 1)
+            ts(A("cs", t * 20, 16), A("b6", 256, 16), -float(RS), OP.add)
+            remote(prev, "lc", t * 20, 17, "cs", t * 20, "rc%d" % t)
+            eq16(u)
+            s_div(u)
+            z_make(u)
+            h_round(u)
+            xrep(u, 2)
+            h_mod(u)
+            s_mod(u)
+            z_ok(u)
+            xrep(u, 3)
+            xrep(u, 4)
+            z_pick(u)
+            z_store(u)
+            for k in range(5, 16):
+                xrep(u, k)
+            weights(u)
+            append_list(t)
+            append_scatter(t)
+            prod(u)
+            floor_place(u, 0)
+            floor_place(u, 1)
+            offsets(u, 0)
+            offsets(u, 1)
+        else:
+            place(u, EARLY, C - EARLY)
+            counts(u)
+            remote(prev, "lc", t * 20 + 16, 1, "cs", t * 20 + 16, "rc%d" % t)
+
+    e = ST - 1
+    dma("Y", T.yx[:, 0:EARLY], T.lx[:, e * C:e * C + EARLY], "oy", 32, [("lx", e * C, e * C + EARLY, None)], [])
+    dma("Y", T.yx[:, EARLY:C], T.lx[:, e * C + EARLY:(e + 1) * C], "oy", 32, [("lx", e * C + EARLY, (e + 1) * C, None)], [])
+    dma("Y", T.yn[:], T.lc[:, e * 20 + 16:e * 20 + 17], "on", 16, [("lc", e * 20 + 16, e * 20 + 17, None)], [])
+    need("Y", ("oy", 32))
+    need("Y", ("on", 16))
+    for k in ("V", "S", "P", "G"):
+        need("G", ("q" + k, cnt[k]))
+    g.wait_ge(T.sem["ls"], local[0])

@@ -1,27 +1,29 @@
 import numpy as np
-from concourse.bass import DstId, RemoteDMATransfer
-from concourse.mybir import dt, AluOpType, AxisListType, ActivationFunctionType
+from concourse.mybir import AluOpType, ActivationFunctionType
 
 OP = AluOpType
 AF = ActivationFunctionType
 C = 256
 RS = 768
 ST = 4
-CH = {"V0": (0, 4, "V"), "S0": (4, 4, "S"), "V1": (8, 4, "V"), "V2": (12, 4, "V")}
+CH = {"V0": (0, 4, "V", "b0", "b4"), "S0": (4, 4, "S", "b1", "b5"), "V1": (8, 4, "V", "b2", "b4"), "V2": (12, 4, "V", "b3", "b5")}
+CHUNKS = tuple(CH)
 EARLY = 192
 XR_S = 6
+PIECES = ((0, 64), (64, 64), (128, 64), (192, 64))
+CYC, PEC, WAKE, SLACK, LOOK = 1.0e-3, 0.71e-3, 0.1, 0.03, 2.0
 
 SCRATCH = {
     "st": ("sbuf", [128, 264], "bfloat16"), "sdv": ("sbuf", [128, 1024], "bfloat16"), "si": ("sbuf", [128, 2], "int32"),
     "l0": ("sbuf", [128, 264], "bfloat16"), "ldv": ("sbuf", [128, 1024], "bfloat16"), "li": ("sbuf", [128, 2], "int32"),
-    "win": ("sbuf", [128, 16 * RS], "bfloat16"),
+    "hst": ("sbuf", [128, 4096], "bfloat16"), "win": ("sbuf", [128, 16 * RS], "bfloat16"),
     "lx": ("sbuf", [128, ST * C], "bfloat16"), "lc": ("sbuf", [128, ST * 20], "float32"), "cs": ("sbuf", [128, ST * 20], "float32"),
     "x": ("sbuf", [128, 5 * C], "bfloat16"), "xr": ("sbuf", [128, ST * 4096], "bfloat16"),
-    "d": ("sbuf", [128, ST * 4096], "bfloat16"), "ad": ("sbuf", [128, ST * 16, 256], "bfloat16"), "yb": ("sbuf", [128, ST * 1024], "bfloat16"),
+    "d": ("sbuf", [128, 2 * 4096], "bfloat16"), "ad": ("sbuf", [128, 2 * 16, 256], "bfloat16"), "yb": ("sbuf", [128, 2 * 4096], "bfloat16"),
     "off": ("sbuf", [128, ST * C], "uint16"), "lu": ("sbuf", [128, ST * 16], "uint16"), "sel": ("sbuf", [128, ST * 16], "uint16"),
     "km": ("sbuf", [128, ST * C], "int32"), "ka": ("sbuf", [128, ST * 16], "int32"),
-    "ax": ("sbuf", [128, 5 * C], "bfloat16"), "gt": ("sbuf", [128, 5 * C], "float16"), "eq": ("sbuf", [128, 5 * C], "float16"),
-    "nn": ("sbuf", [128, 5 * C], "float32"), "pn": ("sbuf", [128, 5 * C], "float16"),
+    "ax": ("sbuf", [128, 5 * C], "bfloat16"), "gp": ("sbuf", [128, 5 * 512], "float16"), "eq": ("sbuf", [128, 5 * C], "float16"),
+    "nn": ("sbuf", [128, 5 * C], "float32"), "rk": ("sbuf", [128, ST * 16], "float32"),
     "sg": ("sbuf", [128, ST * C], "bfloat16"), "sq": ("sbuf", [128, ST * C], "float32"), "hd": ("sbuf", [128, ST * C], "int32"), "h": ("sbuf", [128, ST * C], "int32"),
     "r": ("sbuf", [128, ST * C], "float16"), "sm": ("sbuf", [128, ST * C], "float16"),
     "z": ("sbuf", [128, ST * C], "bfloat16"), "az": ("sbuf", [128, ST * C], "bfloat16"), "okz": ("sbuf", [128, ST * C], "bfloat16"),
@@ -30,14 +32,14 @@ SCRATCH = {
     "v": ("sbuf", [128, ST * C], "float32"), "pp": ("sbuf", [128, ST * C], "float16"), "wn": ("sbuf", [128, ST * 128], "float16"),
     "i3": ("sbuf", [128, 128], "int32"), "i4": ("sbuf", [128, 128], "int32"), "ic": ("sbuf", [128, 256], "int32"), "ip": ("sbuf", [128, 1], "int32"),
     "iq": ("sbuf", [128, 1], "int32"), "t1": ("sbuf", [128, 128], "float32"), "t2": ("sbuf", [128, 128], "float32"), "t3": ("sbuf", [128, 128], "float32"), "t4": ("sbuf", [128, 128], "float32"),
-    "cb": ("sbuf", [128, 7 * 128], "bfloat16"), "cf": ("sbuf", [128, 6 * 128], "float16"),
-    "s4": ("sbuf", [128, 144], "bfloat16"), "s1": ("sbuf", [128, 144], "float16"), "s7": ("sbuf", [128, 144], "float16"),
+    "cb": ("sbuf", [128, 6 * 128], "bfloat16"), "cf": ("sbuf", [128, 6 * 128], "float16"),
+    "s4": ("sbuf", [128, 144], "bfloat16"), "s1": ("sbuf", [128, 144], "float16"),
     "cc": ("sbuf", [128, 256], "bfloat16"), "co": ("sbuf", [128, 64], "int32"), "ia": ("sbuf", [128, 64], "int32"), "k1": ("sbuf", [128, 64], "bfloat16"), "k2": ("sbuf", [128, 64], "bfloat16"),
     "mk": ("sbuf", [128, 64], "float32"), "one": ("sbuf", [128, 256], "float32"), "col": ("sbuf", [128, 32], "float32"),
 }
 for _k in range(8):
     SCRATCH["b%d" % _k] = ("psum", [128, 512], "float32")
-SEMAPHORES = (["qV", "qS", "qP", "qG", "sx", "si", "sdv0", "sdv1", "hs", "rx", "rdv0", "ri", "rdv1", "ls", "oy", "on"]
+SEMAPHORES = (["qV", "qS", "qP", "qG", "sx", "si", "sdv0", "sdv1", "hs0", "hs1", "hs2", "hs3", "rx", "rdv0", "ri", "rdv1", "ls", "oy", "on"]
               + ["%s%d" % (k, t) for k in ("ra", "rb", "rc") for t in range(ST)])
 BONES, NB, ID, NID, I5, I2048 = [128 * k for k in range(6)]
 F1, F768, FI, FD, FM64, FT = [128 * k for k in range(6)]
@@ -53,7 +55,81 @@ def rank_program(g, core, T, topo):
     Q = {"V": g.vector, "S": g.scalar, "P": g.tensor, "G": g, "Y": g.sync}
     cnt = {"V": 0, "S": 0, "P": 0, "G": 0}
     seen = {k: {} for k in Q}
-    clock, hist, local = {}, {}, [0]
+    clock, local = {}, [0]
+    ops, hist = [], {}
+
+    def op(E, call, reads, writes, cost, kind="c", sem=None, val=0, lat=0.0, after=None):
+        j, dep = len(ops), {}
+        for wr, lst in ((False, reads), (True, writes)):
+            for (b, c0, c1, ln) in lst:
+                bank = SCRATCH[b][0] == "psum"
+                for (w, e, a0, a1, l2, i) in hist.get(b, []):
+                    hit = a0 < c1 and c0 < a1 and (ln is None or l2 is None or ln == l2)
+                    if e == E:
+                        if hit and w and E != "P":
+                            dep[i] = True
+                        elif (bank and E == "P") or (hit and (w or wr)):
+                            dep.setdefault(i, False)
+                    elif bank or (hit and (w or wr)):
+                        dep[i] = True
+        if after is not None:
+            dep[after] = False
+        ops.append({"E": E, "call": call, "cost": cost, "kind": kind, "sem": sem, "val": val, "lat": lat, "dep": dep})
+        for wr, lst in ((False, reads), (True, writes)):
+            for (b, c0, c1, ln) in lst:
+                hist.setdefault(b, []).append((wr, "dma" if kind in ("dma", "arr") else E, c0, c1, ln, j))
+        return j
+
+    def schedule():
+        n = len(ops)
+        succ = [[] for _ in range(n)]
+        left = [0] * n
+        for j in range(n):
+            left[j] = len(ops[j]["dep"])
+            for i, w in ops[j]["dep"].items():
+                succ[i].append((j, w))
+        prio = [0.0] * n
+        for j in range(n - 1, -1, -1):
+            o = ops[j]
+            best = 0.0
+            for k, w in succ[j]:
+                best = max(best, prio[k] + (o["cost"] + o["lat"] + WAKE if w or ops[k]["kind"] == "arr" else 0.0))
+            prio[j] = max(best, o["cost"])
+        ready = [0.0] * n
+        pool = {}
+        free = {}
+        for j in range(n):
+            if left[j] == 0:
+                pool.setdefault(ops[j]["E"], []).append(j)
+        order = []
+        while len(order) < n:
+            pick = None
+            for E, lst in pool.items():
+                if lst:
+                    f = 0.0 if E == "N" else free.get(E, 0.0)
+                    te = min(max(f, ready[j]) for j in lst)
+                    if pick is None or te < pick[0]:
+                        pick = (te, E, f)
+            te, E, f = pick
+            lst = pool[E]
+            best = max((j for j in lst if max(f, ready[j]) <= te + SLACK), key=lambda j: (prio[j], -j))
+            end = max(f, ready[best]) + ops[best]["cost"]
+            soon = [j for j in lst if ready[j] < end - 0.02 and prio[j] > prio[best] + LOOK]
+            if soon:
+                best = max(soon, key=lambda j: (prio[j] - max(f, ready[j]), -j))
+            lst.remove(best)
+            o = ops[best]
+            st = max(f, ready[best])
+            free[E] = st + o["cost"]
+            fin = st + o["cost"] + o["lat"]
+            order.append(best)
+            for k, w in succ[best]:
+                r = fin + WAKE if w else (fin if ops[k]["kind"] == "arr" else st)
+                ready[k] = max(ready[k], r)
+                left[k] -= 1
+                if left[k] == 0:
+                    pool.setdefault(ops[k]["E"], []).append(k)
+        return order
 
     def need(E, tok):
         if seen[E].get(tok[0], 0) >= tok[1]:
@@ -63,43 +139,40 @@ def rank_program(g, core, T, topo):
             if seen[E].get(s, 0) < v:
                 seen[E][s] = v
 
-    def deps(E, reads, writes):
-        toks = {}
-        for wr, lst in ((False, reads), (True, writes)):
-            for (b, c0, c1, ln) in lst:
-                bank = SCRATCH[b][0] == "psum"
-                for (w, e, a0, a1, l2, tok) in hist.get(b, []):
-                    hit = a0 < c1 and c0 < a1 and (ln is None or l2 is None or ln == l2)
-                    if e == E:
-                        need_it = hit and E != "P" and w
-                    else:
-                        need_it = bank or (hit and (w or wr))
-                    if need_it and toks.get(tok[0], 0) < tok[1]:
-                        toks[tok[0]] = tok[1]
-        for s in sorted(toks):
-            need(E, (s, toks[s]))
-
-    def note(E, tok, reads, writes):
-        for wr, lst in ((False, reads), (True, writes)):
-            for (b, c0, c1, ln) in lst:
-                hist.setdefault(b, []).append((wr, E, c0, c1, ln, tok))
-
-    def op(E, call, reads, writes):
-        deps(E, reads, writes)
-        cnt[E] += 1
-        tok = ("q" + E, cnt[E])
-        call().then_inc(T.sem[tok[0]], 1)
-        ck = dict(seen[E])
-        ck[tok[0]] = tok[1]
-        clock[tok] = ck
-        note(E, tok, reads, writes)
+    def emit(order):
+        tok = {}
+        for j in order:
+            o = ops[j]
+            E = o["E"]
+            if o["kind"] == "arr":
+                tok[j] = (o["sem"], o["val"])
+                continue
+            want = {}
+            for i, w in o["dep"].items():
+                if w and i in tok:
+                    want[tok[i][0]] = max(want.get(tok[i][0], 0), tok[i][1])
+            for s in sorted(want):
+                need(E, (s, want[s]))
+            if o["kind"] == "c":
+                cnt[E] += 1
+                tk = ("q" + E, cnt[E])
+                o["call"]().then_inc(T.sem[tk[0]], 1)
+                ck = dict(seen[E])
+                ck[tk[0]] = tk[1]
+                clock[tk] = ck
+                tok[j] = tk
+            elif o["kind"] == "dma":
+                o["call"]().then_inc(T.sem[o["sem"]], 16)
+                tok[j] = (o["sem"], o["val"])
+            else:
+                o["call"]()
 
     def A(b, c0=0, n=1, step=1, lane=None):
         ap = T[b][:, c0:c0 + n] if step == 1 else T[b][:, c0:c0 + (n - 1) * step + 1:step]
-        return (ap, [(b, c0, c0 + (n - 1) * step + 1, lane)])
+        return (ap, [(b, c0, c0 + (n - 1) * step + 1, lane)], n)
 
     def ind(win, off):
-        return (win[0].indirect(off[0]), win[1] + off[1])
+        return (win[0].indirect(off[0]), win[1] + off[1], 16 * off[2], "ind")
 
     def sc(s, rd):
         if isinstance(s, tuple):
@@ -107,52 +180,62 @@ def rank_program(g, core, T, topo):
             return s[0]
         return s
 
+    def two(*aps):
+        return all(SCRATCH[a[1][0][0]][2] in ("bfloat16", "float16", "uint16") for a in aps)
+
+    def ps(*aps):
+        return any(SCRATCH[a[1][0][0]][0] == "psum" for a in aps)
+
+    def vc(n):
+        return max(64, n) * CYC
+
     def tt(o, a, b, f):
-        op("V", lambda: g.vector.tensor_tensor(o[0], a[0], b[0], f), a[1] + b[1], o[1])
+        c = 0.05 + 1.5 * o[2] * CYC if len(a) == 4 else vc(o[2] * (1 if ps(a, b) else 2))
+        op("V", lambda: g.vector.tensor_tensor(o[0], a[0], b[0], f), a[1] + b[1], o[1], c)
 
     def ts(o, a, s1, f1, s2=None, f2=None):
         rd = list(a[1])
         p1 = sc(s1, rd)
+        c = vc(o[2] * (0.5 if two(o, a) else 1))
         if f2 is None:
-            op("V", lambda: g.vector.tensor_scalar(o[0], a[0], p1, None, f1), rd, o[1])
+            op("V", lambda: g.vector.tensor_scalar(o[0], a[0], p1, None, f1), rd, o[1], c)
         else:
             p2 = sc(s2, rd)
-            op("V", lambda: g.vector.tensor_scalar(o[0], a[0], p1, p2, f1, f2), rd, o[1])
+            op("V", lambda: g.vector.tensor_scalar(o[0], a[0], p1, p2, f1, f2), rd, o[1], c)
 
     def cp(o, a):
-        op("V", lambda: g.vector.tensor_copy(o[0], a[0]), a[1], o[1])
+        c = 0.05 + 1.5 * o[2] * CYC if len(a) == 4 else 0.05 + 3.5 * a[2] * CYC if len(o) == 4 else vc(o[2] * (0.5 if two(o, a) else 1))
+        rd, wr = (a[1], o[1]) if len(o) == 3 else (a[1] + o[1][1:], o[1][:1])
+        op("V", lambda: g.vector.tensor_copy(o[0], a[0]), rd, wr, c)
 
     def scan(o, d0, d1, init, f0, f1):
         rd = d0[1] + d1[1]
         i0 = sc(init, rd)
-        op("V", lambda: g.vector.tensor_tensor_scan(o[0], d0[0], d1[0], i0, f0, f1), rd, o[1])
+        op("V", lambda: g.vector.tensor_tensor_scan(o[0], d0[0], d1[0], i0, f0, f1), rd, o[1], vc(o[2]))
 
     def act(o, a, f, bias=0.0, scale=1.0):
         rd = list(a[1])
         b0 = sc(bias, rd)
-        op("S", lambda: g.scalar.activation(o[0], a[0], f, b0, scale), rd, o[1])
+        c = 0.065 + 1.5 * o[2] * CYC if len(a) == 4 else vc(o[2])
+        op("S", lambda: g.scalar.activation(o[0], a[0], f, b0, scale), rd, o[1], c)
 
     def mm(o, l, r, start, stop):
-        op("P", lambda: g.tensor.matmul(o[0], l[0], r[0], start, stop), l[1] + r[1], o[1])
+        op("P", lambda: g.tensor.matmul(o[0], l[0], r[0], start, stop), l[1] + r[1], o[1], max(64, r[2]) * PEC)
 
     def mms(o, pairs):
         for k, (l, r) in enumerate(pairs):
             mm(o, l, r, k == 0, k == len(pairs) - 1)
 
-    def dma(E, o_ap, i_ap, sem, total, reads, writes):
-        deps(E, reads, writes)
-        Q[E].dma_start(o_ap, i_ap).then_inc(T.sem[sem], 16)
-        note("dma", (sem, total), reads, writes)
+    def dma(E, o_ap, i_ap, sem, total, reads, writes, us):
+        op(E, lambda: Q[E].dma_start(o_ap, i_ap), reads, writes, 0.1, "dma", sem, total, us)
 
-    def remote(dst, b, c0, n, srcb, s0, rsem):
-        src = A(srcb, s0, n)
-        deps("G", src[1], [])
+    def send(dst, src, b, c0, n, srcb, s0, rsem):
+        s = A(srcb, s0, n)
         rid, pid, _ = topo.addr(dst)
-        g.remote_dma(T[b][:, c0:c0 + n], src[0], T.sem[rsem], T.sem["ls"], pid, rid, topo.mask(core, dst))
+        j = op("G", lambda: g.remote_dma(T[b][:, c0:c0 + n], s[0], T.sem[rsem], T.sem["ls"], pid, rid, topo.mask(core, dst)),
+               s[1], [], 1.0, "rem", lat=1.5 + n * 0.0025)
         local[0] += len(topo.engines(core, dst))
-
-    def arrives(src, b, c0, n, rsem):
-        note("net", (rsem, len(topo.engines(src, core))), [], [(b, c0, c0 + n, None)])
+        op("N", None, [], [(b, c0, c0 + n, None)], 0.0, "arr", rsem, len(topo.engines(src, core)), after=j)
 
     def CB(k):
         return A("cb", k, 128)
@@ -166,34 +249,26 @@ def rank_program(g, core, T, topo):
     def X(t, c0=0, n=C):
         return A("l0", c0, n) if t == 0 else A("x", t * C + c0, n)
 
-    dma("Y", T.st[:, 0:256], T.x0[:], "sx", 32, [], [("st", 0, 256, None)])
-    dma("S", T.st[:, 256:257], T.tg[:], "sx", 32, [], [("st", 256, 257, None)])
-    dma("S", T.si[:, 0:1], T.te[:], "si", 32, [], [("si", 0, 1, None)])
-    dma("S", T.si[:, 1:2], T.cn[:], "si", 32, [], [("si", 1, 2, None)])
-    dma("Y", T.sdv[:, 0:256], T.dv[:, 0:256], "sdv0", 16, [], [("sdv", 0, 256, None)])
-    for q in range(16):
-        dma("Y" if q % 2 == 0 else "S", T.win[:, q * RS:q * RS + 256], T.hs[:, q * 256:(q + 1) * 256], "hs", 256, [], [("win", q * RS, q * RS + 256, None)])
-    dma("Y", T.sdv[:, 256:1024], T.dv[:, 256:1024], "sdv1", 16, [], [("sdv", 256, 1024, None)])
+    dma("Y", T.st[:, 0:256], T.x0[:], "sx", 32, [], [("st", 0, 256, None)], 2.5)
+    dma("S", T.st[:, 256:257], T.tg[:], "sx", 32, [], [("st", 256, 257, None)], 2.5)
+    dma("S", T.si[:, 0:1], T.te[:], "si", 32, [], [("si", 0, 1, None)], 3.0)
+    dma("S", T.si[:, 1:2], T.cn[:], "si", 32, [], [("si", 1, 2, None)], 3.0)
+    dma("Y", T.sdv[:, 0:256], T.dv[:, 0:256], "sdv0", 16, [], [("sdv", 0, 256, None)], 3.0)
+    for k in range(4):
+        dma("Y", T.hst[:, 1024 * k:1024 * k + 1024], T.hs[:, 1024 * k:1024 * k + 1024], "hs%d" % k, 16, [], [("hst", 1024 * k, 1024 * k + 1024, None)], 4.0 + k)
+    dma("Y", T.sdv[:, 256:1024], T.dv[:, 256:1024], "sdv1", 16, [], [("sdv", 256, 1024, None)], 9.0)
 
-    op("G", lambda: g.iota(T.i4[:], [[-16, 8], [0, 16]], 0, 1), [], [("i4", 0, 128, None)])
-    op("G", lambda: g.iota(T.ip[:], [[0, 1]], 0, 1), [], [("ip", 0, 1, None)])
-    op("G", lambda: g.iota(T.i3[:], [[-1, 128]], 0, 1), [], [("i3", 0, 128, None)])
-    op("G", lambda: g.iota(T.ic[:], [[1, 256]], 0, 0), [], [("ic", 0, 256, None)])
-    remote(nxt, "l0", 0, 264 if False else 257, "st", 0, "rx")
-    remote(nxt, "ldv", 0, 256, "sdv", 0, "rdv0")
-    remote(nxt, "li", 0, 2, "si", 0, "ri")
-    remote(nxt, "ldv", 256, 768, "sdv", 256, "rdv1")
-    arrives(prev, "l0", 0, 257, "rx")
-    arrives(prev, "ldv", 0, 256, "rdv0")
-    arrives(prev, "li", 0, 2, "ri")
-    arrives(prev, "ldv", 256, 768, "rdv1")
-    for t in range(ST):
-        arrives(nxt, "lx", t * C, EARLY, "ra%d" % t)
-        arrives(nxt, "lx", t * C + EARLY, C - EARLY, "rb%d" % t)
-        if t < ST - 1:
-            arrives(nxt, "lc", t * 20, 17, "rc%d" % t)
-        else:
-            arrives(nxt, "lc", t * 20 + 16, 1, "rc%d" % t)
+    def iota(b, n, pattern, base, cm):
+        op("G", lambda: g.iota(T[b][:], pattern, base, cm), [], [(b, 0, n, None)], 0.13 + 2 * n * CYC)
+
+    iota("i4", 128, [[-16, 8], [0, 16]], 0, 1)
+    iota("ip", 1, [[0, 1]], 0, 1)
+    iota("i3", 128, [[-1, 128]], 0, 1)
+    iota("ic", 256, [[1, 256]], 0, 0)
+    send(nxt, prev, "l0", 0, 257, "st", 0, "rx")
+    send(nxt, prev, "ldv", 0, 256, "sdv", 0, "rdv0")
+    send(nxt, prev, "li", 0, 2, "si", 0, "ri")
+    send(nxt, prev, "ldv", 256, 768, "sdv", 256, "rdv1")
 
     I3, I4 = A("i3", 0, 128), A("i4", 0, 128)
     T1, T2, T3, T4 = A("t1", 0, 128), A("t2", 0, 128), A("t3", 0, 128), A("t4", 0, 128)
@@ -220,37 +295,41 @@ def rank_program(g, core, T, topo):
     ts(CF(FM64), I3, 0, OP.is_equal, -64.0, OP.mult)
     ts(CB(NB), CB(BONES), -1.0, OP.mult)
     ts(CB(NID), I3, 0, OP.is_equal, -1.0, OP.mult)
-    for b, w in (("s4", 4096.0), ("s1", 1.0), ("s7", float(RS))):
+    for b in ("s4", "s1"):
         ts(A(b, 0, 144), A("ic", 0, 144), 0.0, OP.mult)
     ts(A("co", 0, 64), A("ic", 0, 64), 15, OP.bitwise_and)
     ts(A("ia", 0, 64), A("ic", 0, 64), 4, OP.arith_shift_right)
-    for b, w in (("s4", 4096.0), ("s1", 1.0), ("s7", float(RS))):
+    for b, w in (("s4", 4096.0), ("s1", 1.0)):
         ts(A(b, 15, 8, 16), A("cb", BONES, 8, 16), w, OP.mult)
     ts(A("k2", 0, 64), A("co", 0, 64), COL(Q16), OP.add)
     ts(A("k1", 0, 64), A("ia", 0, 64), 256.0, OP.mult)
     ts(A("mk", 0, 64), A("co", 0, 64), 1.0, OP.min)
-    op("V", lambda: g.vector.memset(T.one[:], 1.0), [], [("one", 0, 256, None)])
+    op("V", lambda: g.vector.memset(T.one[:], 1.0), [], [("one", 0, 256, None)], vc(256))
+    for q in range(16):
+        if q % 4 == 3:
+            act(A("win", q * RS, 256), A("hst", q * 256, 256), AF.Copy)
+        else:
+            cp(A("win", q * RS, 256), A("hst", q * 256, 256))
 
     def absx(t, c0, n):
         act(A("ax", t * C + c0, n), X(t, c0, n), AF.Abs, COL(NTG))
 
     def ring(t, c0, n):
         mms(A("b6", c0, n), [(CB(BONES), A("ax", t * C + c0, n))])
-        ts(A("gt", t * C + c0, n), A("b6", c0, n), COL(THR), OP.is_ge)
-        mms(A("b7", c0, n), [(CF(FD), A("gt", t * C + c0, n))])
+        ts(A("gp", t * 512 + c0, n), A("b6", c0, n), COL(THR), OP.is_ge)
+        mms(A("b7", c0, n), [(CF(FD), A("gp", t * 512 + c0, n))])
 
     def place(t, c0, n):
         scan(A("nn", t * C + c0, n), A("one", 0, n), A("b7", c0, n), COL(NM + t - 1) if c0 == 0 else A("nn", t * C + c0 - 1, 1), OP.mult, OP.add)
         if t < ST:
-            tt(A("pn", t * C + c0, n), A("nn", t * C + c0, n), A("b7", c0, n), OP.mult)
-
-    def list_rings(t):
-        for p in range(16):
-            mm(A("b6", 256, 16), A("s7", 15 - p, 128), A("gt", t * C + p, 16, 16), p == 0, False)
+            tt(A("gp", t * 512 + C + c0, n), A("nn", t * C + c0, n), A("b7", c0, n), OP.mult)
 
     def list_places(t):
         for p in range(16):
-            mm(A("b6", 256, 16), A("s1", 15 - p, 128), A("pn", t * C + p, 16, 16), False, p == 15)
+            mm(A("b6", 256, 32), A("s1", 15 - p, 128), A("gp", t * 512 + p, 32, 16), p == 0, p == 15)
+        rk = A("rk", (t - 1) * 16, 16)
+        ts(rk, A("b6", 256, 16), float(RS), OP.mult, -float(RS), OP.add)
+        tt(A("cs", (t - 1) * 20, 16), rk, A("b6", 272, 16), OP.add)
 
     def counts(t):
         last = A("nn", t * C + C - 1, 1)
@@ -258,244 +337,146 @@ def rank_program(g, core, T, topo):
         if t < ST:
             ts(COL(NM + t), last, 511.0, OP.min)
 
-    def eq16(t):
-        cp(A("eq", t * C, C), A("b7", 0, C))
-
-    def w_first(t):
-        mms(A("b0", 0, C), [(CB(BONES), X(t)), (CB(I5), A("cc", 0, C))])
+    def follow(t):
+        w0 = [(CB(BONES), X(t)), (CB(I5), A("cc", 0, C))]
+        mms(A("b0", 0, C), w0)
         act(A("sg", t * C, C), A("b0", 0, C), AF.Sign, COL(BA + t))
-        mms(A("b1", 0, C), [(CB(BONES), X(t)), (CB(I5), A("cc", 0, C)), (CB(I2048), A("sg", t * C, C))])
-
-    def w_square(t):
-        act(A("sq", t * C, C), A("b1", 0, C), AF.Square, COL(BB + t), 1.0 / 16)
-
-    def h_round(t):
+        mms(A("b0", 256, C), w0 + [(CB(I2048), A("sg", t * C, C))])
+        act(A("sq", t * C, C), A("b0", 256, C), AF.Square, COL(BB + t), 1.0 / 16)
         ts(A("hd", t * C, C), A("sq", t * C, C), 2.0, OP.mult, -4156.0 / 128, OP.add)
-
-    def h_mod(t):
         ts(A("h", t * C, C), A("hd", t * C, C), 4095, OP.bitwise_and)
-
-    def s_div(t):
-        mms(A("b2", 0, C), [(CB(BONES), X(t))])
-        ts(A("r", t * C, C), A("b2", 0, C), 1.0 / 64, OP.mult, 1026.0 - 63.0 / 128, OP.add)
-        mms(A("b2", 256, C), [(CB(BONES), X(t)), (CF(FM64), A("r", t * C, C))])
-
-    def s_mod(t):
-        ts(A("sm", t * C, C), A("b2", 256, C), 1026.0 * 64, OP.add)
-
-    def z_make(t):
-        mms(A("b3", 0, C), [(CB(ID), X(t)), (CB(NID), A("ldv", t * C, C))])
-        act(A("z", t * C, C), A("b3", 0, C), AF.Abs)
+        cp(A("eq", t * C, C), A("b7", 0, C))
+        mms(A("b1", 0, C), [(CB(BONES), X(t))])
+        ts(A("r", t * C, C), A("b1", 0, C), 1.0 / 64, OP.mult, 1026.0 - 63.0 / 128, OP.add)
+        mms(A("b1", 256, C), [(CB(BONES), X(t)), (CF(FM64), A("r", t * C, C))])
+        ts(A("sm", t * C, C), A("b1", 256, C), 1026.0 * 64, OP.add)
+        mms(A("b2", 0, C), [(CB(ID), X(t)), (CB(NID), A("ldv", t * C, C))])
+        act(A("z", t * C, C), A("b2", 0, C), AF.Abs)
         act(A("az", t * C, C), A("z", t * C, C), AF.Abs, COL(NTG))
-
-    def z_ok(t):
-        mms(A("b4", 0, C), [(CB(BONES), A("az", t * C, C)), (CB(NB), A("ax", t * C, C)), (CF(FT), A("sm", t * C, C))])
-        mms(A("b5", 0, C), [(CB(ID), A("z", t * C, C)), (CB(NID), X(t))])
-        ts(A("okz", t * C, C), A("b4", 0, C), 0.0, OP.is_le)
-
-    def z_pick(t):
-        tt(A("pz", t * C, C), A("okz", t * C, C), A("b5", 0, C), OP.mult)
-        mms(A("b3", 256, C), [(CB(ID), X(t)), (CB(ID), A("pz", t * C, C))])
-
-    def z_store(t):
-        act(A("zx", t * C, C), A("b3", 256, C), AF.Copy)
-
-    def xrep(t, k):
-        o = A("xr", t * 4096 + k, C, 16, k)
-        if k < 16 - XR_S:
-            cp(o, X(t))
-        else:
-            act(o, X(t), AF.Copy)
+        mms(A("b3", 0, C), [(CB(BONES), A("az", t * C, C)), (CB(NB), A("ax", t * C, C)), (CF(FT), A("sm", t * C, C))])
+        mms(A("b3", 256, C), [(CB(ID), A("z", t * C, C)), (CB(NID), X(t))])
+        ts(A("okz", t * C, C), A("b3", 0, C), 0.0, OP.is_le)
+        tt(A("pz", t * C, C), A("okz", t * C, C), A("b3", 256, C), OP.mult)
+        mms(A("b2", 256, C), [(CB(ID), X(t)), (CB(ID), A("pz", t * C, C))])
+        act(A("zx", t * C, C), A("b2", 256, C), AF.Copy)
+        for k in range(16):
+            o = A("xr", t * 4096 + k, C, 16, k)
+            if k < 16 - XR_S:
+                cp(o, X(t))
+            else:
+                act(o, X(t), AF.Copy)
 
     def weights(t):
         ts(A("wn", t * 128, 128), CF(F1), COL(N0) if t == 0 else A("lc", (t - 1) * 20 + 16, 1), OP.mult)
-        mms(A("b0", 0, C), [(A("wn", t * 128, 128), A("eq", t * C, C))])
+        mms(A("b4", 0, C), [(A("wn", t * 128, 128), A("eq", t * C, C))])
 
     def append(t):
         cp(A("lu", t * 16, 16), A("lc", t * 20, 16))
         cp(ind(A("win", 0, 16 * RS), A("lu", t * 16, 16)), A("lx", t * C, C))
 
-    def append_list(t):
-        cp(A("lu", t * 16, 16), A("lc", t * 20, 16))
-
-    def append_scatter(t):
-        w, o = A("win", 0, 16 * RS), A("lu", t * 16, 16)
-        src = A("lx", t * C, C)
-        op("V", lambda: g.vector.tensor_copy(w[0].indirect(o[0]), src[0]), src[1] + o[1], w[1])
-
-    def prod(t):
-        tt(A("v", t * C, C), A("h", t * C, C), A("b0", 0, C), OP.mult)
-
-    def floor_place(t, half):
-        c0 = 128 * half
-        ts(A("pp", t * C + c0, 128), A("v", t * C + c0, 128), 1.0 / 4096, OP.mult, 1026.0 - 2047.5 / 4096, OP.add)
-        mms(A("b%d" % (1 + 6 * half), c0, 128), [(CF(FI), A("pp", t * C + c0, 128)), (CF(F768), A("gt", t * C + c0, 128))])
-
-    def offsets(t, half):
-        c0 = 128 * half
-        ts(A("off", t * C + c0, 128), A("b%d" % (1 + 6 * half), c0, 128), -1026.0 - RS, OP.add)
+    def lists(t):
+        for k, (c0, n) in enumerate(PIECES):
+            b = ("b5", "b1", "b0", "b7")[k]
+            tt(A("v", t * C + c0, n), A("h", t * C + c0, n), A("b4", c0, n), OP.mult)
+            ts(A("pp", t * C + c0, n), A("v", t * C + c0, n), 1.0 / 4096, OP.mult, 1026.0 - 2047.5 / 4096, OP.add)
+            mms(A(b, c0, n), [(CF(FI), A("pp", t * C + c0, n)), (CF(F768), A("gp", t * 512 + c0, n))])
+            ts(A("off", t * C + c0, n), A(b, c0, n), -1026.0 - RS, OP.add)
 
     def gather(t, k):
-        a0, al, e = CH[k]
+        a0, al, e = CH[k][:3]
         n = 256 * al
         src = ind(A("win", 0, 16 * RS), A("off", t * C + 16 * a0, 16 * al))
         if e == "V":
-            tt(A("d", t * 4096 + 256 * a0, n), src, A("xr", t * 4096 + 256 * a0, n), OP.subtract)
+            tt(A("d", t % 2 * 4096 + 256 * a0, n), src, A("xr", t * 4096 + 256 * a0, n), OP.subtract)
         else:
-            act(A("yb", t * 1024, n), src, AF.Copy)
+            act(A("yb", t % 2 * 4096 + 256 * a0, n), src, AF.Copy)
 
-    def absd(t, k, lo, hi):
-        a0, al, e = CH[k]
-        for j in range(lo, hi):
-            o = (T.ad[:, t * 16 + a0 + j, :], [("ad", (t * 16 + a0 + j) * 256, (t * 16 + a0 + j + 1) * 256, None)])
+    def absd(t, k):
+        a0, al, e = CH[k][:3]
+        for j in range(al):
+            r = t % 2 * 16 + a0 + j
+            o = (T.ad[:, r, :], [("ad", r * 256, (r + 1) * 256, None)], 256)
             if e == "V":
-                src = A("d", t * 4096 + 256 * (a0 + j), 256)
+                src = A("d", r * 256, 256)
             else:
-                src = A("b%d" % (2 + j // 2), 256 * (j % 2), 256)
+                b = "b%d" % (2 + j // 2 % 2)
+                src = A(b, 256 * (j % 2), 256)
                 if j % 2 == 0:
-                    mms(A("b%d" % (2 + j // 2), 0, 512), [(CB(ID), A("yb", t * 1024 + 256 * j, 512)), (CB(NID), A("xr", t * 4096 + 256 * (a0 + j), 512))])
+                    mms(A(b, 0, 512), [(CB(ID), A("yb", r * 256, 512)), (CB(NID), A("xr", t * 4096 + 256 * (a0 + j), 512))])
             act(o, src, AF.Abs)
 
-    KB = {"V0": "b0", "S0": "b1", "V1": "b0", "V2": "b1"}
-
     def key(t, k):
-        a0, al, e = CH[k]
+        a0, al = CH[k][:2]
         n = 16 * al
-        o = A(KB[k], 0, n)
+        o = A(CH[k][3], 0, n)
+        r = t % 2 * 16 + a0
         mm(o, CB(ID), A("k1", 0, n), True, False)
         mm(o, CB(ID), A("k2", 0, n), False, False)
         for p in range(16):
-            r = (T.ad[:, t * 16 + a0:t * 16 + a0 + al, 16 * p:16 * p + 16], [("ad", (t * 16 + a0) * 256, (t * 16 + a0 + al) * 256, None)])
-            mm(o, A("s4", 15 - p, 128), r, False, p == 15)
+            mm(o, A("s4", 15 - p, 128), (T.ad[:, r:r + al, 16 * p:16 * p + 16], [("ad", r * 256, (r + al) * 256, None)], n), False, p == 15)
 
     def choose(t, k):
-        a0, al, e = CH[k]
+        a0, al, e, kb, db = CH[k]
         n, c0 = 16 * al, t * C + 16 * a0
-        scan(A("km", c0, n), A("mk", 0, n), A(KB[k], 0, n), 0.0, OP.mult, OP.max)
+        w0 = t % 2 * 4096 + 256 * a0
+        scan(A("km", c0, n), A("mk", 0, n), A(kb, 0, n), 0.0, OP.mult, OP.max)
         ts(A("ka", t * 16 + a0, al), A("km", c0 + 15, al, 16), 4095, OP.bitwise_and)
         cp(A("sel", t * 16 + a0, al), A("ka", t * 16 + a0, al))
         if e == "V":
-            tt(A("y", c0, n), ind(A("d", t * 4096 + 256 * a0, 256 * al), A("sel", t * 16 + a0, al)), X(t, 16 * a0, n), OP.add)
+            tt(A("y", c0, n), ind(A("d", w0, 256 * al), A("sel", t * 16 + a0, al)), X(t, 16 * a0, n), OP.add)
         else:
-            cp(A("y", c0, n), ind(A("yb", t * 1024, 256 * al), A("sel", t * 16 + a0, al)))
+            cp(A("y", c0, n), ind(A("yb", w0, 256 * al), A("sel", t * 16 + a0, al)))
         act(A("ay", c0, n), A("y", c0, n), AF.Abs, COL(NTG))
-        mms(A("b4", 16 * a0, n), [(CB(NB), A("ax", c0, n)), (CF(FT), A("sm", c0, n)), (CB(BONES), A("ay", c0, n))])
-        mms(A("b5", 16 * a0, n), [(CB(ID), A("y", c0, n)), (CB(NID), A("zx", c0, n))])
-        mms(A("b5", 256 + 16 * a0, n), [(CB(ID), A("zx", c0, n))])
-
-    def decide(t, k):
-        a0, al, e = CH[k]
-        n, c0 = 16 * al, t * C + 16 * a0
-        ts(A("oky", c0, n), A("b4", 16 * a0, n), 0.0, OP.is_le)
-        tt(A("pr", c0, n), A("oky", c0, n), A("b5", 16 * a0, n), OP.mult)
-        tt(X(t + 1, 16 * a0, n), A("pr", c0, n), A("b5", 256 + 16 * a0, n), OP.add)
-        if t < ST or True:
-            absx(t + 1, 16 * a0, n)
+        mms(A(db, 0, n), [(CB(NB), A("ax", c0, n)), (CF(FT), A("sm", c0, n)), (CB(BONES), A("ay", c0, n))])
+        mms(A(db, 128, n), [(CB(ID), A("y", c0, n)), (CB(NID), A("zx", c0, n))])
+        mms(A(db, 256, n), [(CB(ID), A("zx", c0, n))])
+        ts(A("oky", c0, n), A(db, 0, n), 0.0, OP.is_le)
+        tt(A("pr", c0, n), A("oky", c0, n), A(db, 128, n), OP.mult)
+        tt(X(t + 1, 16 * a0, n), A("pr", c0, n), A(db, 256, n), OP.add)
+        absx(t + 1, 16 * a0, n)
 
     ts(COL(NTG), A("l0", 256, 1), -1.0, OP.mult)
     cp(COL(N0), A("si", 1, 1))
+    cp(COL(TT), A("li", 0, 1))
+    ts(COL(NM), A("li", 1, 1), -1.0, OP.add)
+    ts(CF(FT), CB(ID), COL(TT), OP.mult, -1.0, OP.mult)
     absx(0, 0, C)
-    w_first(0)
-    for k in range(16 - XR_S):
-        if k < 2:
-            xrep(0, k)
     ring(0, 0, C)
-    w_square(0)
-    eq16(0)
+    follow(0)
     weights(0)
-    h_round(0)
-    h_mod(0)
-    prod(0)
-    floor_place(0, 0)
-    floor_place(0, 1)
-    for k in range(2, 16):
-        xrep(0, k)
-    offsets(0, 0)
-    offsets(0, 1)
-
-    def z_part(t):
-        s_div(t)
-        z_make(t)
-        s_mod(t)
-        z_ok(t)
-        z_pick(t)
-        z_store(t)
+    lists(0)
 
     for t in range(ST):
-        gather(t, "V0")
-        gather(t, "S0")
-        if t == 0:
-            cp(COL(TT), A("li", 0, 1))
-            ts(COL(NM), A("li", 1, 1), -1.0, OP.add)
-            ts(CF(FT), CB(ID), COL(TT), OP.mult, -1.0, OP.mult)
-        gather(t, "V1")
-        absd(t, "V0", 0, 4)
-        key(t, "V0")
-        if t == 0:
-            z_part(0)
-        absd(t, "S0", 0, 4)
-        key(t, "S0")
-        choose(t, "V0")
-        gather(t, "V2")
-        absd(t, "V1", 0, 4)
-        decide(t, "V0")
-        key(t, "V1")
-        absd(t, "V2", 0, 4)
-        choose(t, "S0")
-        choose(t, "V1")
-        decide(t, "S0")
-        key(t, "V2")
-        decide(t, "V1")
-        remote(prev, "lx", t * C, EARLY, "x", (t + 1) * C, "ra%d" % t)
         u = t + 1
-        ring(u, 0, EARLY)
-        choose(t, "V2")
-        place(u, 0, EARLY)
-        decide(t, "V2")
-        remote(prev, "lx", t * C + EARLY, C - EARLY, "x", u * C + EARLY, "rb%d" % t)
+        for k in CHUNKS:
+            gather(t, k)
+        for k in CHUNKS:
+            absd(t, k)
+            key(t, k)
+            choose(t, k)
+            if 16 * (CH[k][0] + CH[k][1]) == EARLY:
+                send(prev, nxt, "lx", t * C, EARLY, "x", u * C, "ra%d" % t)
+                ring(u, 0, EARLY)
+                place(u, 0, EARLY)
+        send(prev, nxt, "lx", t * C + EARLY, C - EARLY, "x", u * C + EARLY, "rb%d" % t)
         ring(u, EARLY, C - EARLY)
+        place(u, EARLY, C - EARLY)
+        counts(u)
         if u < ST:
-            list_rings(u)
-            w_first(u)
-            xrep(u, 0)
-            place(u, EARLY, C - EARLY)
             list_places(u)
-            counts(u)
-            w_square(u)
-            xrep(u, 1)
-            ts(A("cs", t * 20, 16), A("b6", 256, 16), -float(RS), OP.add)
-            remote(prev, "lc", t * 20, 17, "cs", t * 20, "rc%d" % t)
-            eq16(u)
-            s_div(u)
-            z_make(u)
-            h_round(u)
-            xrep(u, 2)
-            h_mod(u)
-            s_mod(u)
-            z_ok(u)
-            xrep(u, 3)
-            xrep(u, 4)
-            z_pick(u)
-            z_store(u)
-            for k in range(5, 16):
-                xrep(u, k)
+            send(prev, nxt, "lc", t * 20, 17, "cs", t * 20, "rc%d" % t)
+            follow(u)
             weights(u)
-            append_list(t)
-            append_scatter(t)
-            prod(u)
-            floor_place(u, 0)
-            floor_place(u, 1)
-            offsets(u, 0)
-            offsets(u, 1)
+            append(t)
+            lists(u)
         else:
-            place(u, EARLY, C - EARLY)
-            counts(u)
-            remote(prev, "lc", t * 20 + 16, 1, "cs", t * 20 + 16, "rc%d" % t)
+            send(prev, nxt, "lc", t * 20 + 16, 1, "cs", t * 20 + 16, "rc%d" % t)
 
     e = ST - 1
-    dma("Y", T.yx[:, 0:EARLY], T.lx[:, e * C:e * C + EARLY], "oy", 32, [("lx", e * C, e * C + EARLY, None)], [])
-    dma("Y", T.yx[:, EARLY:C], T.lx[:, e * C + EARLY:(e + 1) * C], "oy", 32, [("lx", e * C + EARLY, (e + 1) * C, None)], [])
-    dma("Y", T.yn[:], T.lc[:, e * 20 + 16:e * 20 + 17], "on", 16, [("lc", e * 20 + 16, e * 20 + 17, None)], [])
+    dma("Y", T.yx[:, 0:EARLY], T.lx[:, e * C:e * C + EARLY], "oy", 32, [("lx", e * C, e * C + EARLY, None)], [], 2.0)
+    dma("Y", T.yx[:, EARLY:C], T.lx[:, e * C + EARLY:(e + 1) * C], "oy", 32, [("lx", e * C + EARLY, (e + 1) * C, None)], [], 2.0)
+    dma("Y", T.yn[:], T.lc[:, e * 20 + 16:e * 20 + 17], "on", 16, [("lc", e * 20 + 16, e * 20 + 17, None)], [], 2.0)
+    emit(schedule())
     need("Y", ("oy", 32))
     need("Y", ("on", 16))
     for k in ("V", "S", "P", "G"):

import numpy as np
from concourse.mybir import AluOpType, ActivationFunctionType

OP = AluOpType
AF = ActivationFunctionType
C = 256
RS = 768
ST = 4
CH = {"V0": (0, 4, "V", "b0", "b4"), "S0": (4, 4, "S", "b1", "b5"), "V1": (8, 4, "V", "b2", "b4"), "V2": (12, 4, "V", "b3", "b5")}
CHUNKS = tuple(CH)
EARLY = 192
XR_S = 6
PIECES = ((0, 64), (64, 64), (128, 64), (192, 64))
CYC, PEC, WAKE, SLACK, LOOK = 1.0e-3, 0.71e-3, 0.1, 0.03, 2.0

SCRATCH = {
    "st": ("sbuf", [128, 264], "bfloat16"), "sdv": ("sbuf", [128, 1024], "bfloat16"), "si": ("sbuf", [128, 2], "int32"),
    "l0": ("sbuf", [128, 264], "bfloat16"), "ldv": ("sbuf", [128, 1024], "bfloat16"), "li": ("sbuf", [128, 2], "int32"),
    "hst": ("sbuf", [128, 4096], "bfloat16"), "win": ("sbuf", [128, 16 * RS], "bfloat16"),
    "lx": ("sbuf", [128, ST * C], "bfloat16"), "lc": ("sbuf", [128, ST * 20], "float32"), "cs": ("sbuf", [128, ST * 20], "float32"),
    "x": ("sbuf", [128, 5 * C], "bfloat16"), "xr": ("sbuf", [128, ST * 4096], "bfloat16"),
    "d": ("sbuf", [128, 2 * 4096], "bfloat16"), "ad": ("sbuf", [128, 2 * 16, 256], "bfloat16"), "yb": ("sbuf", [128, 2 * 4096], "bfloat16"),
    "off": ("sbuf", [128, ST * C], "uint16"), "lu": ("sbuf", [128, ST * 16], "uint16"), "sel": ("sbuf", [128, ST * 16], "uint16"),
    "km": ("sbuf", [128, ST * C], "int32"), "ka": ("sbuf", [128, ST * 16], "int32"),
    "ax": ("sbuf", [128, 5 * C], "bfloat16"), "gp": ("sbuf", [128, 5 * 512], "float16"), "eq": ("sbuf", [128, 5 * C], "float16"),
    "nn": ("sbuf", [128, 5 * C], "float32"), "rk": ("sbuf", [128, ST * 16], "float32"),
    "sg": ("sbuf", [128, ST * C], "bfloat16"), "sq": ("sbuf", [128, ST * C], "float32"), "hd": ("sbuf", [128, ST * C], "int32"), "h": ("sbuf", [128, ST * C], "int32"),
    "r": ("sbuf", [128, ST * C], "float16"), "sm": ("sbuf", [128, ST * C], "float16"),
    "z": ("sbuf", [128, ST * C], "bfloat16"), "az": ("sbuf", [128, ST * C], "bfloat16"), "okz": ("sbuf", [128, ST * C], "bfloat16"),
    "pz": ("sbuf", [128, ST * C], "bfloat16"), "zx": ("sbuf", [128, ST * C], "bfloat16"),
    "y": ("sbuf", [128, ST * C], "bfloat16"), "ay": ("sbuf", [128, ST * C], "bfloat16"), "oky": ("sbuf", [128, ST * C], "bfloat16"), "pr": ("sbuf", [128, ST * C], "bfloat16"),
    "v": ("sbuf", [128, ST * C], "float32"), "pp": ("sbuf", [128, ST * C], "float16"), "wn": ("sbuf", [128, ST * 128], "float16"),
    "i3": ("sbuf", [128, 128], "int32"), "i4": ("sbuf", [128, 128], "int32"), "ic": ("sbuf", [128, 256], "int32"), "ip": ("sbuf", [128, 1], "int32"),
    "iq": ("sbuf", [128, 1], "int32"), "t1": ("sbuf", [128, 128], "float32"), "t2": ("sbuf", [128, 128], "float32"), "t3": ("sbuf", [128, 128], "float32"), "t4": ("sbuf", [128, 128], "float32"),
    "cb": ("sbuf", [128, 6 * 128], "bfloat16"), "cf": ("sbuf", [128, 6 * 128], "float16"),
    "s4": ("sbuf", [128, 144], "bfloat16"), "s1": ("sbuf", [128, 144], "float16"),
    "cc": ("sbuf", [128, 256], "bfloat16"), "co": ("sbuf", [128, 64], "int32"), "ia": ("sbuf", [128, 64], "int32"), "k1": ("sbuf", [128, 64], "bfloat16"), "k2": ("sbuf", [128, 64], "bfloat16"),
    "mk": ("sbuf", [128, 64], "float32"), "one": ("sbuf", [128, 256], "float32"), "col": ("sbuf", [128, 32], "float32"),
}
for _k in range(8):
    SCRATCH["b%d" % _k] = ("psum", [128, 512], "float32")
SEMAPHORES = (["qV", "qS", "qP", "qG", "sx", "si", "sdv0", "sdv1", "hs0", "hs1", "hs2", "hs3", "rx", "rdv0", "ri", "rdv1", "ls", "oy", "on"]
              + ["%s%d" % (k, t) for k in ("ra", "rb", "rc") for t in range(ST)])
BONES, NB, ID, NID, I5, I2048 = [128 * k for k in range(6)]
F1, F768, FI, FD, FM64, FT = [128 * k for k in range(6)]
NTG, THR, TT, N0, NM, BA, BB, Q16 = 0, 1, 2, 3, 4, 12, 16, 20


def rank_program(g, core, T, topo):
    rank = T.rank_of(core)
    if rank is None:
        return
    N = len(T.cores)
    prev, nxt = T.cores[(rank - 1) % N], T.cores[(rank + 1) % N]
    Q = {"V": g.vector, "S": g.scalar, "P": g.tensor, "G": g, "Y": g.sync}
    cnt = {"V": 0, "S": 0, "P": 0, "G": 0}
    seen = {k: {} for k in Q}
    clock, local = {}, [0]
    ops, hist = [], {}

    def op(E, call, reads, writes, cost, kind="c", sem=None, val=0, lat=0.0, after=None):
        j, dep = len(ops), {}
        for wr, lst in ((False, reads), (True, writes)):
            for (b, c0, c1, ln) in lst:
                bank = SCRATCH[b][0] == "psum"
                for (w, e, a0, a1, l2, i) in hist.get(b, []):
                    hit = a0 < c1 and c0 < a1 and (ln is None or l2 is None or ln == l2)
                    if e == E:
                        if hit and w and E != "P":
                            dep[i] = True
                        elif (bank and E == "P") or (hit and (w or wr)):
                            dep.setdefault(i, False)
                    elif bank or (hit and (w or wr)):
                        dep[i] = True
        if after is not None:
            dep[after] = False
        ops.append({"E": E, "call": call, "cost": cost, "kind": kind, "sem": sem, "val": val, "lat": lat, "dep": dep})
        for wr, lst in ((False, reads), (True, writes)):
            for (b, c0, c1, ln) in lst:
                hist.setdefault(b, []).append((wr, "dma" if kind in ("dma", "arr") else E, c0, c1, ln, j))
        return j

    def schedule():
        n = len(ops)
        succ = [[] for _ in range(n)]
        left = [0] * n
        for j in range(n):
            left[j] = len(ops[j]["dep"])
            for i, w in ops[j]["dep"].items():
                succ[i].append((j, w))
        prio = [0.0] * n
        for j in range(n - 1, -1, -1):
            o = ops[j]
            best = 0.0
            for k, w in succ[j]:
                best = max(best, prio[k] + (o["cost"] + o["lat"] + WAKE if w or ops[k]["kind"] == "arr" else 0.0))
            prio[j] = max(best, o["cost"])
        ready = [0.0] * n
        pool = {}
        free = {}
        for j in range(n):
            if left[j] == 0:
                pool.setdefault(ops[j]["E"], []).append(j)
        order = []
        while len(order) < n:
            pick = None
            for E, lst in pool.items():
                if lst:
                    f = 0.0 if E == "N" else free.get(E, 0.0)
                    te = min(max(f, ready[j]) for j in lst)
                    if pick is None or te < pick[0]:
                        pick = (te, E, f)
            te, E, f = pick
            lst = pool[E]
            best = max((j for j in lst if max(f, ready[j]) <= te + SLACK), key=lambda j: (prio[j], -j))
            end = max(f, ready[best]) + ops[best]["cost"]
            soon = [j for j in lst if ready[j] < end - 0.02 and prio[j] > prio[best] + LOOK]
            if soon:
                best = max(soon, key=lambda j: (prio[j] - max(f, ready[j]), -j))
            lst.remove(best)
            o = ops[best]
            st = max(f, ready[best])
            free[E] = st + o["cost"]
            fin = st + o["cost"] + o["lat"]
            order.append(best)
            for k, w in succ[best]:
                r = fin + WAKE if w else (fin if ops[k]["kind"] == "arr" else st)
                ready[k] = max(ready[k], r)
                left[k] -= 1
                if left[k] == 0:
                    pool.setdefault(ops[k]["E"], []).append(k)
        return order

    def need(E, tok):
        if seen[E].get(tok[0], 0) >= tok[1]:
            return
        Q[E].wait_ge(T.sem[tok[0]], tok[1])
        for s, v in clock.get(tok, {tok[0]: tok[1]}).items():
            if seen[E].get(s, 0) < v:
                seen[E][s] = v

    def emit(order):
        tok = {}
        for j in order:
            o = ops[j]
            E = o["E"]
            if o["kind"] == "arr":
                tok[j] = (o["sem"], o["val"])
                continue
            want = {}
            for i, w in o["dep"].items():
                if w and i in tok:
                    want[tok[i][0]] = max(want.get(tok[i][0], 0), tok[i][1])
            for s in sorted(want):
                need(E, (s, want[s]))
            if o["kind"] == "c":
                cnt[E] += 1
                tk = ("q" + E, cnt[E])
                o["call"]().then_inc(T.sem[tk[0]], 1)
                ck = dict(seen[E])
                ck[tk[0]] = tk[1]
                clock[tk] = ck
                tok[j] = tk
            elif o["kind"] == "dma":
                o["call"]().then_inc(T.sem[o["sem"]], 16)
                tok[j] = (o["sem"], o["val"])
            else:
                o["call"]()

    def A(b, c0=0, n=1, step=1, lane=None):
        ap = T[b][:, c0:c0 + n] if step == 1 else T[b][:, c0:c0 + (n - 1) * step + 1:step]
        return (ap, [(b, c0, c0 + (n - 1) * step + 1, lane)], n)

    def ind(win, off):
        return (win[0].indirect(off[0]), win[1] + off[1], 16 * off[2], "ind")

    def sc(s, rd):
        if isinstance(s, tuple):
            rd.extend(s[1])
            return s[0]
        return s

    def two(*aps):
        return all(SCRATCH[a[1][0][0]][2] in ("bfloat16", "float16", "uint16") for a in aps)

    def ps(*aps):
        return any(SCRATCH[a[1][0][0]][0] == "psum" for a in aps)

    def vc(n):
        return max(64, n) * CYC

    def tt(o, a, b, f):
        c = 0.05 + 1.5 * o[2] * CYC if len(a) == 4 else vc(o[2] * (1 if ps(a, b) else 2))
        op("V", lambda: g.vector.tensor_tensor(o[0], a[0], b[0], f), a[1] + b[1], o[1], c)

    def ts(o, a, s1, f1, s2=None, f2=None):
        rd = list(a[1])
        p1 = sc(s1, rd)
        c = vc(o[2] * (0.5 if two(o, a) else 1))
        if f2 is None:
            op("V", lambda: g.vector.tensor_scalar(o[0], a[0], p1, None, f1), rd, o[1], c)
        else:
            p2 = sc(s2, rd)
            op("V", lambda: g.vector.tensor_scalar(o[0], a[0], p1, p2, f1, f2), rd, o[1], c)

    def cp(o, a):
        c = 0.05 + 1.5 * o[2] * CYC if len(a) == 4 else 0.05 + 3.5 * a[2] * CYC if len(o) == 4 else vc(o[2] * (0.5 if two(o, a) else 1))
        rd, wr = (a[1], o[1]) if len(o) == 3 else (a[1] + o[1][1:], o[1][:1])
        op("V", lambda: g.vector.tensor_copy(o[0], a[0]), rd, wr, c)

    def scan(o, d0, d1, init, f0, f1):
        rd = d0[1] + d1[1]
        i0 = sc(init, rd)
        op("V", lambda: g.vector.tensor_tensor_scan(o[0], d0[0], d1[0], i0, f0, f1), rd, o[1], vc(o[2]))

    def act(o, a, f, bias=0.0, scale=1.0):
        rd = list(a[1])
        b0 = sc(bias, rd)
        c = 0.065 + 1.5 * o[2] * CYC if len(a) == 4 else vc(o[2])
        op("S", lambda: g.scalar.activation(o[0], a[0], f, b0, scale), rd, o[1], c)

    def mm(o, l, r, start, stop):
        op("P", lambda: g.tensor.matmul(o[0], l[0], r[0], start, stop), l[1] + r[1], o[1], max(64, r[2]) * PEC)

    def mms(o, pairs):
        for k, (l, r) in enumerate(pairs):
            mm(o, l, r, k == 0, k == len(pairs) - 1)

    def dma(E, o_ap, i_ap, sem, total, reads, writes, us):
        op(E, lambda: Q[E].dma_start(o_ap, i_ap), reads, writes, 0.1, "dma", sem, total, us)

    def send(dst, src, b, c0, n, srcb, s0, rsem):
        s = A(srcb, s0, n)
        rid, pid, _ = topo.addr(dst)
        j = op("G", lambda: g.remote_dma(T[b][:, c0:c0 + n], s[0], T.sem[rsem], T.sem["ls"], pid, rid, topo.mask(core, dst)),
               s[1], [], 1.0, "rem", lat=1.5 + n * 0.0025)
        local[0] += len(topo.engines(core, dst))
        op("N", None, [], [(b, c0, c0 + n, None)], 0.0, "arr", rsem, len(topo.engines(src, core)), after=j)

    def CB(k):
        return A("cb", k, 128)

    def CF(k):
        return A("cf", k, 128)

    def COL(k):
        return A("col", k, 1)

    def X(t, c0=0, n=C):
        return A("l0", c0, n) if t == 0 else A("x", t * C + c0, n)

    dma("Y", T.st[:, 0:256], T.x0[:], "sx", 32, [], [("st", 0, 256, None)], 2.5)
    dma("S", T.st[:, 256:257], T.tg[:], "sx", 32, [], [("st", 256, 257, None)], 2.5)
    dma("S", T.si[:, 0:1], T.te[:], "si", 32, [], [("si", 0, 1, None)], 3.0)
    dma("S", T.si[:, 1:2], T.cn[:], "si", 32, [], [("si", 1, 2, None)], 3.0)
    dma("Y", T.sdv[:, 0:256], T.dv[:, 0:256], "sdv0", 16, [], [("sdv", 0, 256, None)], 3.0)
    for k in range(4):
        dma("Y", T.hst[:, 1024 * k:1024 * k + 1024], T.hs[:, 1024 * k:1024 * k + 1024], "hs%d" % k, 16, [], [("hst", 1024 * k, 1024 * k + 1024, None)], 4.0 + k)
    dma("Y", T.sdv[:, 256:1024], T.dv[:, 256:1024], "sdv1", 16, [], [("sdv", 256, 1024, None)], 9.0)

    def iota(b, n, pattern, base, cm):
        op("G", lambda: g.iota(T[b][:], pattern, base, cm), [], [(b, 0, n, None)], 0.13 + 2 * n * CYC)

    iota("i4", 128, [[-16, 8], [0, 16]], 0, 1)
    iota("ip", 1, [[0, 1]], 0, 1)
    iota("i3", 128, [[-1, 128]], 0, 1)
    iota("ic", 256, [[1, 256]], 0, 0)
    send(nxt, prev, "l0", 0, 257, "st", 0, "rx")
    send(nxt, prev, "ldv", 0, 256, "sdv", 0, "rdv0")
    send(nxt, prev, "li", 0, 2, "si", 0, "ri")
    send(nxt, prev, "ldv", 256, 768, "sdv", 256, "rdv1")

    I3, I4 = A("i3", 0, 128), A("i4", 0, 128)
    T1, T2, T3, T4 = A("t1", 0, 128), A("t2", 0, 128), A("t3", 0, 128), A("t4", 0, 128)
    IQ = A("iq", 0, 1)
    ts(T1, I4, 0, OP.is_ge)
    ts(T2, I4, 15, OP.is_le)
    ts(IQ, A("ip", 0, 1), 15, OP.bitwise_and)
    tt(CB(BONES), T1, T2, OP.mult)
    ts(CB(ID), I3, 0, OP.is_equal)
    ts(CB(I5), I3, 0, OP.is_equal, 5.0, OP.mult)
    ts(CB(I2048), I3, 0, OP.is_equal, -2048.0, OP.mult)
    cp(A("cc", 0, 256), A("ic", 0, 256))
    ts(COL(THR), IQ, 128.0, OP.mult)
    for t in range(ST):
        ts(COL(BA + t), IQ, -97.0, OP.mult, 1455.0 + 31 * t - 4095.5, OP.add)
        ts(COL(BB + t), IQ, -97.0 / 16, OP.mult, (1455.0 + 31 * t - 2048 + 64) / 16, OP.add)
    ts(COL(Q16), IQ, 16.0, OP.mult)
    ts(T3, I3, 1, OP.is_equal, -1.0, OP.mult)
    ts(CF(F1), CB(BONES), 1.0, OP.mult)
    tt(T4, T3, CB(BONES), OP.mult)
    ts(CF(F768), CB(BONES), float(RS), OP.mult)
    ts(CF(FI), I3, 0, OP.is_equal)
    tt(CF(FD), T4, CB(ID), OP.add)
    ts(CF(FM64), I3, 0, OP.is_equal, -64.0, OP.mult)
    ts(CB(NB), CB(BONES), -1.0, OP.mult)
    ts(CB(NID), I3, 0, OP.is_equal, -1.0, OP.mult)
    for b in ("s4", "s1"):
        ts(A(b, 0, 144), A("ic", 0, 144), 0.0, OP.mult)
    ts(A("co", 0, 64), A("ic", 0, 64), 15, OP.bitwise_and)
    ts(A("ia", 0, 64), A("ic", 0, 64), 4, OP.arith_shift_right)
    for b, w in (("s4", 4096.0), ("s1", 1.0)):
        ts(A(b, 15, 8, 16), A("cb", BONES, 8, 16), w, OP.mult)
    ts(A("k2", 0, 64), A("co", 0, 64), COL(Q16), OP.add)
    ts(A("k1", 0, 64), A("ia", 0, 64), 256.0, OP.mult)
    ts(A("mk", 0, 64), A("co", 0, 64), 1.0, OP.min)
    op("V", lambda: g.vector.memset(T.one[:], 1.0), [], [("one", 0, 256, None)], vc(256))
    for q in range(16):
        if q % 4 == 3:
            act(A("win", q * RS, 256), A("hst", q * 256, 256), AF.Copy)
        else:
            cp(A("win", q * RS, 256), A("hst", q * 256, 256))

    def absx(t, c0, n):
        act(A("ax", t * C + c0, n), X(t, c0, n), AF.Abs, COL(NTG))

    def ring(t, c0, n):
        mms(A("b6", c0, n), [(CB(BONES), A("ax", t * C + c0, n))])
        ts(A("gp", t * 512 + c0, n), A("b6", c0, n), COL(THR), OP.is_ge)
        mms(A("b7", c0, n), [(CF(FD), A("gp", t * 512 + c0, n))])

    def place(t, c0, n):
        scan(A("nn", t * C + c0, n), A("one", 0, n), A("b7", c0, n), COL(NM + t - 1) if c0 == 0 else A("nn", t * C + c0 - 1, 1), OP.mult, OP.add)
        if t < ST:
            tt(A("gp", t * 512 + C + c0, n), A("nn", t * C + c0, n), A("b7", c0, n), OP.mult)

    def list_places(t):
        for p in range(16):
            mm(A("b6", 256, 32), A("s1", 15 - p, 128), A("gp", t * 512 + p, 32, 16), p == 0, p == 15)
        rk = A("rk", (t - 1) * 16, 16)
        ts(rk, A("b6", 256, 16), float(RS), OP.mult, -float(RS), OP.add)
        tt(A("cs", (t - 1) * 20, 16), rk, A("b6", 272, 16), OP.add)

    def counts(t):
        last = A("nn", t * C + C - 1, 1)
        ts(A("cs", (t - 1) * 20 + 16, 1), last, 1.0, OP.add, 512.0, OP.min)
        if t < ST:
            ts(COL(NM + t), last, 511.0, OP.min)

    def follow(t):
        w0 = [(CB(BONES), X(t)), (CB(I5), A("cc", 0, C))]
        mms(A("b0", 0, C), w0)
        act(A("sg", t * C, C), A("b0", 0, C), AF.Sign, COL(BA + t))
        mms(A("b0", 256, C), w0 + [(CB(I2048), A("sg", t * C, C))])
        act(A("sq", t * C, C), A("b0", 256, C), AF.Square, COL(BB + t), 1.0 / 16)
        ts(A("hd", t * C, C), A("sq", t * C, C), 2.0, OP.mult, -4156.0 / 128, OP.add)
        ts(A("h", t * C, C), A("hd", t * C, C), 4095, OP.bitwise_and)
        cp(A("eq", t * C, C), A("b7", 0, C))
        mms(A("b1", 0, C), [(CB(BONES), X(t))])
        ts(A("r", t * C, C), A("b1", 0, C), 1.0 / 64, OP.mult, 1026.0 - 63.0 / 128, OP.add)
        mms(A("b1", 256, C), [(CB(BONES), X(t)), (CF(FM64), A("r", t * C, C))])
        ts(A("sm", t * C, C), A("b1", 256, C), 1026.0 * 64, OP.add)
        mms(A("b2", 0, C), [(CB(ID), X(t)), (CB(NID), A("ldv", t * C, C))])
        act(A("z", t * C, C), A("b2", 0, C), AF.Abs)
        act(A("az", t * C, C), A("z", t * C, C), AF.Abs, COL(NTG))
        mms(A("b3", 0, C), [(CB(BONES), A("az", t * C, C)), (CB(NB), A("ax", t * C, C)), (CF(FT), A("sm", t * C, C))])
        mms(A("b3", 256, C), [(CB(ID), A("z", t * C, C)), (CB(NID), X(t))])
        ts(A("okz", t * C, C), A("b3", 0, C), 0.0, OP.is_le)
        tt(A("pz", t * C, C), A("okz", t * C, C), A("b3", 256, C), OP.mult)
        mms(A("b2", 256, C), [(CB(ID), X(t)), (CB(ID), A("pz", t * C, C))])
        act(A("zx", t * C, C), A("b2", 256, C), AF.Copy)
        for k in range(16):
            o = A("xr", t * 4096 + k, C, 16, k)
            if k < 16 - XR_S:
                cp(o, X(t))
            else:
                act(o, X(t), AF.Copy)

    def weights(t):
        ts(A("wn", t * 128, 128), CF(F1), COL(N0) if t == 0 else A("lc", (t - 1) * 20 + 16, 1), OP.mult)
        mms(A("b4", 0, C), [(A("wn", t * 128, 128), A("eq", t * C, C))])

    def append(t):
        cp(A("lu", t * 16, 16), A("lc", t * 20, 16))
        cp(ind(A("win", 0, 16 * RS), A("lu", t * 16, 16)), A("lx", t * C, C))

    def lists(t):
        for k, (c0, n) in enumerate(PIECES):
            b = ("b5", "b1", "b0", "b7")[k]
            tt(A("v", t * C + c0, n), A("h", t * C + c0, n), A("b4", c0, n), OP.mult)
            ts(A("pp", t * C + c0, n), A("v", t * C + c0, n), 1.0 / 4096, OP.mult, 1026.0 - 2047.5 / 4096, OP.add)
            mms(A(b, c0, n), [(CF(FI), A("pp", t * C + c0, n)), (CF(F768), A("gp", t * 512 + c0, n))])
            ts(A("off", t * C + c0, n), A(b, c0, n), -1026.0 - RS, OP.add)

    def gather(t, k):
        a0, al, e = CH[k][:3]
        n = 256 * al
        src = ind(A("win", 0, 16 * RS), A("off", t * C + 16 * a0, 16 * al))
        if e == "V":
            tt(A("d", t % 2 * 4096 + 256 * a0, n), src, A("xr", t * 4096 + 256 * a0, n), OP.subtract)
        else:
            act(A("yb", t % 2 * 4096 + 256 * a0, n), src, AF.Copy)

    def absd(t, k):
        a0, al, e = CH[k][:3]
        for j in range(al):
            r = t % 2 * 16 + a0 + j
            o = (T.ad[:, r, :], [("ad", r * 256, (r + 1) * 256, None)], 256)
            if e == "V":
                src = A("d", r * 256, 256)
            else:
                b = "b%d" % (2 + j // 2 % 2)
                src = A(b, 256 * (j % 2), 256)
                if j % 2 == 0:
                    mms(A(b, 0, 512), [(CB(ID), A("yb", r * 256, 512)), (CB(NID), A("xr", t * 4096 + 256 * (a0 + j), 512))])
            act(o, src, AF.Abs)

    def key(t, k):
        a0, al = CH[k][:2]
        n = 16 * al
        o = A(CH[k][3], 0, n)
        r = t % 2 * 16 + a0
        mm(o, CB(ID), A("k1", 0, n), True, False)
        mm(o, CB(ID), A("k2", 0, n), False, False)
        for p in range(16):
            mm(o, A("s4", 15 - p, 128), (T.ad[:, r:r + al, 16 * p:16 * p + 16], [("ad", r * 256, (r + al) * 256, None)], n), False, p == 15)

    def choose(t, k):
        a0, al, e, kb, db = CH[k]
        n, c0 = 16 * al, t * C + 16 * a0
        w0 = t % 2 * 4096 + 256 * a0
        scan(A("km", c0, n), A("mk", 0, n), A(kb, 0, n), 0.0, OP.mult, OP.max)
        ts(A("ka", t * 16 + a0, al), A("km", c0 + 15, al, 16), 4095, OP.bitwise_and)
        cp(A("sel", t * 16 + a0, al), A("ka", t * 16 + a0, al))
        if e == "V":
            tt(A("y", c0, n), ind(A("d", w0, 256 * al), A("sel", t * 16 + a0, al)), X(t, 16 * a0, n), OP.add)
        else:
            cp(A("y", c0, n), ind(A("yb", w0, 256 * al), A("sel", t * 16 + a0, al)))
        act(A("ay", c0, n), A("y", c0, n), AF.Abs, COL(NTG))
        mms(A(db, 0, n), [(CB(NB), A("ax", c0, n)), (CF(FT), A("sm", c0, n)), (CB(BONES), A("ay", c0, n))])
        mms(A(db, 128, n), [(CB(ID), A("y", c0, n)), (CB(NID), A("zx", c0, n))])
        mms(A(db, 256, n), [(CB(ID), A("zx", c0, n))])
        ts(A("oky", c0, n), A(db, 0, n), 0.0, OP.is_le)
        tt(A("pr", c0, n), A("oky", c0, n), A(db, 128, n), OP.mult)
        tt(X(t + 1, 16 * a0, n), A("pr", c0, n), A(db, 256, n), OP.add)
        absx(t + 1, 16 * a0, n)

    ts(COL(NTG), A("l0", 256, 1), -1.0, OP.mult)
    cp(COL(N0), A("si", 1, 1))
    cp(COL(TT), A("li", 0, 1))
    ts(COL(NM), A("li", 1, 1), -1.0, OP.add)
    ts(CF(FT), CB(ID), COL(TT), OP.mult, -1.0, OP.mult)
    absx(0, 0, C)
    ring(0, 0, C)
    follow(0)
    weights(0)
    lists(0)

    for t in range(ST):
        u = t + 1
        for k in CHUNKS:
            gather(t, k)
        for k in CHUNKS:
            absd(t, k)
            key(t, k)
            choose(t, k)
            if 16 * (CH[k][0] + CH[k][1]) == EARLY:
                send(prev, nxt, "lx", t * C, EARLY, "x", u * C, "ra%d" % t)
                ring(u, 0, EARLY)
                place(u, 0, EARLY)
        send(prev, nxt, "lx", t * C + EARLY, C - EARLY, "x", u * C + EARLY, "rb%d" % t)
        ring(u, EARLY, C - EARLY)
        place(u, EARLY, C - EARLY)
        counts(u)
        if u < ST:
            list_places(u)
            send(prev, nxt, "lc", t * 20, 17, "cs", t * 20, "rc%d" % t)
            follow(u)
            weights(u)
            append(t)
            lists(u)
        else:
            send(prev, nxt, "lc", t * 20 + 16, 1, "cs", t * 20 + 16, "rc%d" % t)

    e = ST - 1
    dma("Y", T.yx[:, 0:EARLY], T.lx[:, e * C:e * C + EARLY], "oy", 32, [("lx", e * C, e * C + EARLY, None)], [], 2.0)
    dma("Y", T.yx[:, EARLY:C], T.lx[:, e * C + EARLY:(e + 1) * C], "oy", 32, [("lx", e * C + EARLY, (e + 1) * C, None)], [], 2.0)
    dma("Y", T.yn[:], T.lc[:, e * 20 + 16:e * 20 + 17], "on", 16, [("lc", e * 20 + 16, e * 20 + 17, None)], [], 2.0)
    emit(schedule())
    need("Y", ("oy", 32))
    need("Y", ("on", 16))
    for k in ("V", "S", "P", "G"):
        need("G", ("q" + k, cnt[k]))
    g.wait_ge(T.sem["ls"], local[0])
